import numpy as np
import ml_dtypes


def mxq(x, axis, fmt="e4m3"):
    dtype, down = {"e4m3": (ml_dtypes.float8_e4m3fn, 7), "e5m2": (ml_dtypes.float8_e5m2, 14)}[fmt]
    v = np.moveaxis(np.asarray(x, np.float32).astype(ml_dtypes.bfloat16).astype(np.float64), axis, -1)
    blocks = v.reshape(v.shape[:-1] + (-1, 32))
    amax = np.abs(blocks).max(-1, keepdims=True)
    byte = np.maximum(np.where(amax > 0, np.frexp(amax)[1] - 1 + 127, 0) - down, 1)
    scale = np.exp2(byte - 127.0)
    codes = (blocks / scale).astype(np.float32).astype(dtype).astype(np.float64)
    return np.moveaxis((codes * scale).reshape(v.shape), -1, axis)


WIDE = False


def mx_kscale(k):
    if not WIDE:
        return np.ones(k)
    levels = np.array([10, -10, 5, -5, 0])
    if k % 512:
        return np.exp2(np.random.permutation(np.resize(levels, k // 32))).repeat(32)
    a = np.empty((k // 512, 16))
    for p in range(k // 512):
        a[p, :8] = np.random.permutation(np.resize(levels, 8))
        for g in range(8):
            far = levels[np.abs(levels - a[p, g]) >= 10]
            a[p, g + 8] = far[np.random.randint(len(far))]
    return np.exp2(a.ravel()).repeat(32)


def f64(x):
    return np.asarray(x).astype(np.float64)


def striped(idx):
    return np.tile(idx.reshape(-1, 16).T, (8, 1)).astype(np.uint16)


def unstriped(offs):
    return offs[:16].T.reshape(-1).astype(np.int64)


E2M1 = np.array([0.0, 0.5, 1.0, 1.5, 2.0, 3.0, 4.0, 6.0, -0.0, -0.5, -1.0, -1.5, -2.0, -3.0, -4.0, -6.0])


def pack_weight(w, fmt):
    k, n = w.shape
    w = f64(np.asarray(w, np.float32).astype(ml_dtypes.bfloat16)).reshape(k // 32, 32, n)
    amax = np.abs(w).max(1)
    if fmt == "e4m3":
        byte = np.frexp(amax)[1] - 1 + 127 - 7
    else:
        mant, ex = np.frexp(amax / 6.0)
        byte = np.where(mant > 0.5, ex, ex - 1) + 127
    byte = np.clip(np.where(amax > 0, byte, 1), 1, 254)
    scaled = (w * np.exp2(127.0 - byte)[:, None, :]).reshape(k, n).astype(np.float32)
    by_word = np.ascontiguousarray(scaled.reshape(k // 512, 128, 4, n).transpose(0, 1, 3, 2))
    if fmt == "e4m3":
        words = by_word.astype(ml_dtypes.float8_e4m3fn).view(np.uint8)
    else:
        c = by_word.astype(ml_dtypes.float4_e2m1fn).view(np.uint8) & 0xF
        words = (c[..., 0::2] | (c[..., 1::2] << 4)).reshape(k // 512, 128, 2 * n)
    return np.ascontiguousarray(words), np.ascontiguousarray(byte.astype(np.uint8).reshape(k // 512, 16, n))


def unpack_weight(words, scales, fmt):
    g, _, n = scales.shape
    words = np.ascontiguousarray(words).reshape(g, 128, n, -1)
    if fmt == "e4m3":
        vals = words.view(ml_dtypes.float8_e4m3fn).astype(np.float64)
    else:
        nib = np.empty((g, 128, n, 4), np.uint8)
        nib[..., 0::2] = words & 0xF
        nib[..., 1::2] = words >> 4
        vals = E2M1[nib]
    vals = vals * np.repeat(np.exp2(scales.astype(np.float64) - 127.0), 8, axis=1)[..., None]
    return vals.transpose(0, 1, 3, 2).reshape(g * 512, n)


K, T, E, C, H, N = 512, 1024, 8, 256, 512, 256


def by_expert(wq, xq):
    return np.concatenate([wq[e].T @ xq[:, e * C:(e + 1) * C] for e in range(E)], axis=1)


def setup_inputs():
    n = np.random.standard_normal
    s = mx_kscale(K)
    u = mx_kscale(H)
    slot_token = np.concatenate([np.random.permutation(T)[:C] for e in range(E)])
    x = pack_weight(n((K, T)) * s[:, None], "e4m3")
    w = [pack_weight(m, "e2m1") for m in n((E, K, N)) / np.sqrt(K) / s[None, :, None]]
    wa = [pack_weight(m, "e4m3") for m in n((E, K, H)) / np.sqrt(K) / s[None, :, None] * u]
    return {
        "x_words": x[0],
        "x_scales": x[1],
        "w_words": np.stack([m[0] for m in w]),
        "w_scales": np.stack([m[1] for m in w]),
        "wa_words": np.stack([m[0] for m in wa]),
        "wa_scales": np.stack([m[1] for m in wa]),
        "wb": (n((E, H, N)) / np.sqrt(H) / u[None, :, None]).astype(np.float32),
        "offs": striped(slot_token),
    }


def reference(x_words, x_scales, w_words, w_scales, wa_words, wa_scales, wb, offs):
    w = np.stack([unpack_weight(w_words[e], w_scales[e], "e2m1") for e in range(E)])
    wa = np.stack([unpack_weight(wa_words[e], wa_scales[e], "e4m3") for e in range(E)])
    wbq = mxq(f64(wb), 1, "e4m3")
    idx = unstriped(offs)
    xq = unpack_weight(x_words, x_scales, "e4m3")[:, idx]
    h = by_expert(wa, xq)
    y = by_expert(w, xq) + by_expert(wbq, mxq(h, 0, "e4m3"))
    out = y
    return out

@@ -1,0 +1,224 @@
+from contextlib import ExitStack
+
+import concourse.mybir as mybir
+
+K, T, E, C, H, N = 512, 1024, 8, 256, 512, 256
+FLOPS = 2 * E * C * (K * H + K * N + H * N)
+
+F32 = mybir.dt.float32
+BF16 = mybir.dt.bfloat16
+I32 = mybir.dt.int32
+U32 = mybir.dt.uint32
+U16 = mybir.dt.uint16
+U8 = mybir.dt.uint8
+FP8X4 = mybir.dt.float8_e4m3fn_x4
+FP4X4 = mybir.dt.float4_e2m1fn_x4
+
+P = 128
+PACK = 4
+HALF = 128
+SET = 4
+LEAD = 2
+SCALAR_CASTS = (0, 1, 2, 3, 4)
+
+
+def tile_moe_elr_s_none_kernel(
+    tc, x_words, x_scales, w_words, w_scales, wa_words, wa_scales, wb, offs, out
+):
+    nc = tc.nc
+    with ExitStack() as ctx:
+        keep = ctx.enter_context(tc.tile_pool(name="keep", bufs=1))
+        slots = ctx.enter_context(tc.tile_pool(name="slots", bufs=8))
+        shared = ctx.enter_context(tc.tile_pool(name="shared", bufs=1))
+        ring = ctx.enter_context(tc.tile_pool(name="ring", bufs=8))
+        h_psum = ctx.enter_context(tc.psum_pool(name="h_psum", bufs=6))
+        y_psum = ctx.enter_context(tc.psum_pool(name="y_psum", bufs=2))
+
+        offsets = keep.tile([P, E * C // 16], U16, name="offsets")
+        x_table = keep.tile([P, T], I32, name="x_table", align_bytes=64)
+        x_rows = keep.tile([P, T // 4], I32, name="x_rows", align_bytes=64)
+        x_plane = keep.tile([P, T], U8, name="x_plane", align_bytes=64)
+        wa_plane_raw = [keep.tile([P, H], U8, name="wa_plane_raw%d" % s, align_bytes=64) for s in range(E // SET)]
+        wa_plane = [keep.tile([P, H], U8, name="wa_plane%d" % s, align_bytes=64) for s in range(E // SET)]
+        w_plane = keep.tile([P, E, N], U8, name="w_plane", align_bytes=64)
+        w_codes = [keep.tile([P, SET, 2 * N], U8, name="w_codes%d" % s, align_bytes=64) for s in range(E // SET)]
+        wa_raw = [shared.tile([P, H], I32, name="wa_raw%d" % e, align_bytes=64, offset=4 * H * e) for e in range(E)]
+        wb_raw = [keep.tile([P, PACK, N], F32, name="wb_raw%d" % e, align_bytes=64) for e in range(E)]
+
+        nc.vector.memset(wa_plane_raw[0][:].bitcast(I32), 0)
+        nc.vector.memset(x_plane[:].bitcast(I32), 0)
+        nc.vector.memset(wa_plane_raw[1][:].bitcast(I32), 0)
+        nc.vector.memset(w_plane[:].bitcast(I32), 0)
+
+        def load_x_plane():
+            for r in range(4):
+                nc.sync.dma_start(x_rows[r:P:32, :], x_scales[0, r:16:4, :].bitcast(I32))
+
+        def load_wa_plane(s):
+            for q in range(4):
+                nc.sync.dma_start(
+                    wa_plane_raw[s][32 * q : 32 * q + 16, :].bitcast(I32),
+                    wa_scales[SET * s : SET * (s + 1), 0, 4 * q : 4 * q + 4, :].bitcast(I32),
+                )
+
+        def load_w_plane():
+            for r in range(4):
+                nc.sync.dma_start(
+                    w_plane[r:P:32, :, :].bitcast(I32),
+                    w_scales[:, 0, r:16:4, :].rearrange("e q n -> q e n").bitcast(I32),
+                )
+
+        def load_w(s):
+            nc.sync.dma_start(
+                w_codes[s][:].bitcast(I32),
+                w_words[SET * s : SET * (s + 1), 0].rearrange("e p b -> p e b").bitcast(I32),
+            )
+
+        def load_wa(e):
+            nc.sync.dma_start(wa_raw[e][:], wa_words[e, 0].rearrange("p i d -> p (i d)").bitcast(I32))
+
+        def load_wb(e):
+            nc.sync.dma_start(wb_raw[e][:], wb[e].rearrange("(p j) n -> p j n", j=PACK))
+
+        load_x_plane()
+        nc.sync.dma_start(offsets[:], offs)
+        nc.sync.dma_start(x_table[:], x_words[0].rearrange("p t d -> p (t d)").bitcast(I32))
+        load_wa(0)
+        load_wb(0)
+        load_wa_plane(0)
+        load_wa(1)
+        load_wb(1)
+        load_w_plane()
+        load_w(0)
+        load_wa(2)
+        load_wb(2)
+        load_wa(3)
+        load_wa_plane(1)
+        load_wb(3)
+        load_wa(4)
+        load_wb(4)
+        load_wa(5)
+        load_w(1)
+        load_wb(5)
+        load_wa(6)
+        load_wa(7)
+        load_wb(6)
+        load_wb(7)
+
+        for q in range(4):
+            nc.vector.tensor_copy(x_plane[32 * q : 32 * q + 4, :].bitcast(I32), x_rows[32 * q : 32 * q + 4, :])
+
+        out_view = out.rearrange("(t p) s -> p t s", p=P)
+        state = {}
+
+        def gather(e):
+            place = 4 * H * ((e - LEAD) % (E + LEAD))
+            xg = shared.tile([P, C], U32, name="xg%d" % e, align_bytes=64, offset=place)
+            xs = shared.tile([P, C], U8, name="xs%d" % e, align_bytes=64, offset=place + 4 * C)
+            lst = offsets[:, e * C // 16 : (e + 1) * C // 16]
+            nc.vector.tensor_copy(xg[:], x_table[:].bitcast(U32).indirect(lst))
+            nc.vector.tensor_copy(xs[:], x_plane[:].indirect(lst))
+            state["x", e] = (xg, xs)
+
+        def permute(e):
+            if e % SET == 0:
+                s = e // SET
+                nc.vector.tensor_copy(
+                    wa_plane[s][:].rearrange("p (t m) -> p m t", t=PACK),
+                    wa_plane_raw[s][:].rearrange("p (m t) -> p m t", t=PACK),
+                )
+            wa = ring.tile([P, H], I32, name="wa", align_bytes=64)
+            nc.vector.tensor_copy(
+                wa[:].rearrange("p (t m) -> p m t", t=PACK),
+                wa_raw[e][:].rearrange("p (m t) -> p m t", t=PACK),
+            )
+            state["wa", e] = wa
+
+        def first_product(e):
+            xg, xs = state["x", e]
+            wa = state["wa", e]
+            plane = wa_plane[e // SET]
+            row = 4 * (e % SET)
+            h_bf = ring.tile([P, C, PACK], BF16, name="h_bf", align_bytes=64)
+            for u in range(C // HALF):
+                cols = slice(u * HALF, (u + 1) * HALF)
+                acc = h_psum.tile([P, PACK, HALF], F32, name="h_acc")
+                for t in range(PACK):
+                    nc.tensor.matmul_mx(
+                        out=acc[:, t, :],
+                        lhsT=wa[:, t * P : (t + 1) * P].bitcast(FP8X4),
+                        lhsT_scale=plane[row:P, t * P : (t + 1) * P],
+                        rhs=xg[:, cols].bitcast(FP8X4),
+                        rhs_scale=xs[:, cols],
+                        start=True,
+                        stop=True,
+                    )
+                nc.scalar.copy(h_bf[:, cols, :], acc[:].rearrange("p t s -> p s t"))
+            state["h_bf", e] = h_bf
+
+        def cast_wb(e):
+            wb_bf = ring.tile([P, N, PACK], BF16, name="wb_bf", align_bytes=64)
+            dst = wb_bf[:].rearrange("p (c i) j -> p c j i", i=4)
+            src = wb_raw[e][:].rearrange("p j (c i) -> p c j i", i=4)
+            if e in SCALAR_CASTS:
+                nc.scalar.copy(dst, src)
+            else:
+                nc.vector.tensor_copy(dst, src)
+            state["wb_bf", e] = wb_bf
+
+        def quantise(name, e, width):
+            codes = ring.tile([P, width], U32, name=name + "_codes", align_bytes=64)
+            plane = ring.tile([P, width], U8, name=name + "_plane", align_bytes=64)
+            nc.vector.quantize_mx(
+                out=codes[:].bitcast(FP8X4),
+                scales=plane[:],
+                in_=state[name + "_bf", e][:].rearrange("p c j -> p (c j)"),
+            )
+            state[name, e] = (codes, plane)
+
+        def second_product(e):
+            xg, xs = state["x", e]
+            hq, hs = state["h", e]
+            bq, bs = state["wb", e]
+            acc = y_psum.tile([P, N // P, C], F32, name="y_acc")
+            for b in range(N // P):
+                rows = slice(b * P, (b + 1) * P)
+                for u in range(C // HALF):
+                    cols = slice(u * HALF, (u + 1) * HALF)
+                    nc.tensor.matmul_mx(
+                        out=acc[:, b, cols],
+                        lhsT=w_codes[e // SET][:, e % SET, 2 * b * P : 2 * (b + 1) * P].bitcast(FP4X4),
+                        lhsT_scale=w_plane[:, e, rows],
+                        rhs=xg[:, cols].bitcast(FP8X4),
+                        rhs_scale=xs[:, cols],
+                        start=True,
+                        stop=False,
+                    )
+                    nc.tensor.matmul_mx(
+                        out=acc[:, b, cols],
+                        lhsT=bq[:, rows].bitcast(FP8X4),
+                        lhsT_scale=bs[:, rows],
+                        rhs=hq[:, cols].bitcast(FP8X4),
+                        rhs_scale=hs[:, cols],
+                        start=False,
+                        stop=True,
+                    )
+            y = keep.tile([P, N // P, C], F32, name="y%d" % e)
+            nc.scalar.copy(y[:], acc[:])
+            nc.sync.dma_start(out_view[:, :, e * C : (e + 1) * C], y[:])
+
+        gather(0)
+        for step in range(E + 2):
+            if step < E:
+                permute(step)
+                if step == 0:
+                    gather(1)
+                cast_wb(step)
+                first_product(step)
+            if 1 <= step <= E:
+                quantise("wb", step - 1, N)
+                quantise("h", step - 1, C)
+            if step + LEAD < E:
+                gather(step + LEAD)
+            if step >= 2:
+                second_product(step - 2)

@@ -16,56 +16,56 @@ FP4X4 = mybir.dt.float4_e2m1fn_x4
 
 P = 128
 PACK = 4
+QUADRANT = 32
+ROWS = 4
 HALF = 128
 SET = 4
-LEAD = 2
-SCALAR_CASTS = (0, 1, 2, 3, 4)
+LEAD = 3
+LAG = 2
+SCALAR_ROUNDS = 6
+H_BANKS, Y_BANKS = 6, 2
+ROOM = C + N + LEAD * C * (1 + PACK)
+ALIGN = 64
 
 
 def tile_moe_elr_s_none_kernel(
     tc, x_words, x_scales, w_words, w_scales, wa_words, wa_scales, wb, offs, out
 ):
     nc = tc.nc
+    sets = range(E // SET)
     with ExitStack() as ctx:
         keep = ctx.enter_context(tc.tile_pool(name="keep", bufs=1))
-        slots = ctx.enter_context(tc.tile_pool(name="slots", bufs=8))
-        shared = ctx.enter_context(tc.tile_pool(name="shared", bufs=1))
-        ring = ctx.enter_context(tc.tile_pool(name="ring", bufs=8))
-        h_psum = ctx.enter_context(tc.psum_pool(name="h_psum", bufs=6))
-        y_psum = ctx.enter_context(tc.psum_pool(name="y_psum", bufs=2))
+        rooms = ctx.enter_context(tc.tile_pool(name="rooms", bufs=1))
+        each = ctx.enter_context(tc.tile_pool(name="each", bufs=E))
+        h_psum = ctx.enter_context(tc.psum_pool(name="h_psum", bufs=H_BANKS))
+        y_psum = ctx.enter_context(tc.psum_pool(name="y_psum", bufs=Y_BANKS))
 
         offsets = keep.tile([P, E * C // 16], U16, name="offsets")
-        x_table = keep.tile([P, T], I32, name="x_table", align_bytes=64)
-        x_rows = keep.tile([P, T // 4], I32, name="x_rows", align_bytes=64)
-        x_plane = keep.tile([P, T], U8, name="x_plane", align_bytes=64)
-        wa_plane_raw = [keep.tile([P, H], U8, name="wa_plane_raw%d" % s, align_bytes=64) for s in range(E // SET)]
-        wa_plane = [keep.tile([P, H], U8, name="wa_plane%d" % s, align_bytes=64) for s in range(E // SET)]
-        w_plane = keep.tile([P, E, N], U8, name="w_plane", align_bytes=64)
-        w_codes = [keep.tile([P, SET, 2 * N], U8, name="w_codes%d" % s, align_bytes=64) for s in range(E // SET)]
-        wa_raw = [shared.tile([P, H], I32, name="wa_raw%d" % e, align_bytes=64, offset=4 * H * e) for e in range(E)]
-        wb_raw = [keep.tile([P, PACK, N], F32, name="wb_raw%d" % e, align_bytes=64) for e in range(E)]
+        x_table = keep.tile([P, T], I32, name="x_table", align_bytes=ALIGN)
+        x_rows = keep.tile([P, T // 4], I32, name="x_rows", align_bytes=ALIGN)
+        x_plane = keep.tile([P, T], U8, name="x_plane", align_bytes=ALIGN)
+        wa_plane_raw = [keep.tile([P, H], U8, name="wa_plane_raw%d" % s, align_bytes=ALIGN) for s in sets]
+        wa_plane = [keep.tile([P, H], U8, name="wa_plane%d" % s, align_bytes=ALIGN) for s in sets]
+        w_plane = keep.tile([P, E, N], U8, name="w_plane", align_bytes=ALIGN)
+        w_codes = [keep.tile([P, SET, 2 * N], U8, name="w_codes%d" % s, align_bytes=ALIGN) for s in sets]
+        wa_raw = [rooms.tile([P, H], I32, name="wa_raw%d" % e, align_bytes=ALIGN, offset=ROOM * e) for e in range(E)]
+        wb_raw = [keep.tile([P, PACK, N], F32, name="wb_raw%d" % e, align_bytes=ALIGN) for e in range(E)]
 
-        nc.vector.memset(wa_plane_raw[0][:].bitcast(I32), 0)
-        nc.vector.memset(x_plane[:].bitcast(I32), 0)
-        nc.vector.memset(wa_plane_raw[1][:].bitcast(I32), 0)
-        nc.vector.memset(w_plane[:].bitcast(I32), 0)
-
-        def load_x_plane():
-            for r in range(4):
-                nc.sync.dma_start(x_rows[r:P:32, :], x_scales[0, r:16:4, :].bitcast(I32))
+        for plane in (wa_plane_raw[0], x_plane, wa_plane_raw[1], w_plane):
+            nc.vector.memset(plane[:].bitcast(I32), 0)
 
         def load_wa_plane(s):
-            for q in range(4):
+            for q in range(ROWS):
                 nc.sync.dma_start(
-                    wa_plane_raw[s][32 * q : 32 * q + 16, :].bitcast(I32),
-                    wa_scales[SET * s : SET * (s + 1), 0, 4 * q : 4 * q + 4, :].bitcast(I32),
+                    wa_plane_raw[s][QUADRANT * q : QUADRANT * q + SET * ROWS, :].bitcast(I32),
+                    wa_scales[SET * s : SET * (s + 1), 0, ROWS * q : ROWS * (q + 1), :].bitcast(I32),
                 )
 
         def load_w_plane():
-            for r in range(4):
+            for r in range(ROWS):
                 nc.sync.dma_start(
-                    w_plane[r:P:32, :, :].bitcast(I32),
-                    w_scales[:, 0, r:16:4, :].rearrange("e q n -> q e n").bitcast(I32),
+                    w_plane[r:P:QUADRANT, :, :].bitcast(I32),
+                    w_scales[:, 0, r : ROWS * ROWS : ROWS, :].rearrange("e q n -> q e n").bitcast(I32),
                 )
 
         def load_w(s):
@@ -80,145 +80,136 @@ def tile_moe_elr_s_none_kernel(
         def load_wb(e):
             nc.sync.dma_start(wb_raw[e][:], wb[e].rearrange("(p j) n -> p j n", j=PACK))
 
-        load_x_plane()
+        for r in range(ROWS):
+            nc.sync.dma_start(x_rows[r:P:QUADRANT, :], x_scales[0, r : ROWS * ROWS : ROWS, :].bitcast(I32))
         nc.sync.dma_start(offsets[:], offs)
         nc.sync.dma_start(x_table[:], x_words[0].rearrange("p t d -> p (t d)").bitcast(I32))
-        load_wa(0)
-        load_wb(0)
+        for e in range(LAG):
+            load_wb(e)
         load_wa_plane(0)
-        load_wa(1)
-        load_wb(1)
-        load_w_plane()
-        load_w(0)
-        load_wa(2)
-        load_wb(2)
-        load_wa(3)
-        load_wa_plane(1)
-        load_wb(3)
-        load_wa(4)
-        load_wb(4)
-        load_wa(5)
-        load_w(1)
-        load_wb(5)
-        load_wa(6)
-        load_wa(7)
-        load_wb(6)
-        load_wb(7)
+        for e in range(E):
+            load_wa(e)
+            if e == LAG:
+                load_w_plane()
+            if e % SET == LAG:
+                load_w(e // SET)
+            if e + 1 == SET:
+                load_wa_plane(1)
+            if e + LAG < SCALAR_ROUNDS:
+                load_wb(e + LAG)
+        for e in range(SCALAR_ROUNDS, E):
+            load_wb(e)
 
-        for q in range(4):
-            nc.vector.tensor_copy(x_plane[32 * q : 32 * q + 4, :].bitcast(I32), x_rows[32 * q : 32 * q + 4, :])
+        for q in range(ROWS):
+            live = slice(QUADRANT * q, QUADRANT * q + ROWS)
+            nc.vector.tensor_copy(x_plane[live, :].bitcast(I32), x_rows[live, :])
 
-        out_view = out.rearrange("(t p) s -> p t s", p=P)
-        state = {}
+        out_view = out.rearrange("(b p) s -> p b s", p=P)
+        slot_words, slot_plane, wa_codes, rounded, quantised = {}, {}, {}, {}, {}
 
-        def gather(e):
-            place = 4 * H * ((e - LEAD) % (E + LEAD))
-            xg = shared.tile([P, C], U32, name="xg%d" % e, align_bytes=64, offset=place)
-            xs = shared.tile([P, C], U8, name="xs%d" % e, align_bytes=64, offset=place + 4 * C)
-            lst = offsets[:, e * C // 16 : (e + 1) * C // 16]
-            nc.vector.tensor_copy(xg[:], x_table[:].bitcast(U32).indirect(lst))
-            nc.vector.tensor_copy(xs[:], x_plane[:].indirect(lst))
-            state["x", e] = (xg, xs)
+        def gather(first, end, room):
+            width = (end - first) * C
+            place = ROOM * room + C + N
+            scale_bytes = rooms.tile([P, width], U8, name="slot_plane%d" % first, align_bytes=ALIGN, offset=place)
+            words = rooms.tile([P, width], U32, name="slot_words%d" % first, align_bytes=ALIGN, offset=place + width)
+            entries = offsets[:, first * C // 16 : end * C // 16]
+            nc.vector.tensor_copy(words[:], x_table[:].bitcast(U32).indirect(entries))
+            nc.vector.tensor_copy(scale_bytes[:], x_plane[:].indirect(entries))
+            for e in range(first, end):
+                own = slice((e - first) * C, (e - first + 1) * C)
+                slot_words[e] = words[:, own]
+                slot_plane[e] = scale_bytes[:, own]
 
         def permute(e):
             if e % SET == 0:
-                s = e // SET
                 nc.vector.tensor_copy(
-                    wa_plane[s][:].rearrange("p (t m) -> p m t", t=PACK),
-                    wa_plane_raw[s][:].rearrange("p (m t) -> p m t", t=PACK),
+                    wa_plane[e // SET][:].rearrange("p (t c i) -> p c t i", t=PACK, i=16),
+                    wa_plane_raw[e // SET][:].rearrange("p (c i t) -> p c t i", t=PACK, i=16),
                 )
-            wa = ring.tile([P, H], I32, name="wa", align_bytes=64)
+            wa_codes[e] = each.tile([P, H], I32, name="wa_codes", align_bytes=ALIGN)
             nc.vector.tensor_copy(
-                wa[:].rearrange("p (t m) -> p m t", t=PACK),
-                wa_raw[e][:].rearrange("p (m t) -> p m t", t=PACK),
+                wa_codes[e][:].rearrange("p (t c i) -> p c t i", t=PACK, i=4),
+                wa_raw[e][:].rearrange("p (c i t) -> p c t i", t=PACK, i=4),
             )
-            state["wa", e] = wa
+
+        def round_wb(e):
+            rounded[e] = each.tile([P, C + N, PACK], BF16, name="rounded", align_bytes=ALIGN)
+            copy = nc.scalar.copy if e < SCALAR_ROUNDS else nc.vector.tensor_copy
+            copy(
+                rounded[e][:, C:, :].rearrange("p (c i) j -> p c j i", i=4),
+                wb_raw[e][:].rearrange("p j (c i) -> p c j i", i=4),
+            )
 
         def first_product(e):
-            xg, xs = state["x", e]
-            wa = state["wa", e]
-            plane = wa_plane[e // SET]
-            row = 4 * (e % SET)
-            h_bf = ring.tile([P, C, PACK], BF16, name="h_bf", align_bytes=64)
-            for u in range(C // HALF):
-                cols = slice(u * HALF, (u + 1) * HALF)
-                acc = h_psum.tile([P, PACK, HALF], F32, name="h_acc")
+            first_row = ROWS * (e % SET)
+            for lo in range(0, C, HALF):
+                slots = slice(lo, lo + HALF)
+                h_sums = h_psum.tile([P, PACK, HALF], F32, name="h_sums")
                 for t in range(PACK):
+                    columns = slice(t * P, (t + 1) * P)
                     nc.tensor.matmul_mx(
-                        out=acc[:, t, :],
-                        lhsT=wa[:, t * P : (t + 1) * P].bitcast(FP8X4),
-                        lhsT_scale=plane[row:P, t * P : (t + 1) * P],
-                        rhs=xg[:, cols].bitcast(FP8X4),
-                        rhs_scale=xs[:, cols],
+                        out=h_sums[:, t, :],
+                        lhsT=wa_codes[e][:, columns].bitcast(FP8X4),
+                        lhsT_scale=wa_plane[e // SET][first_row:P, columns],
+                        rhs=slot_words[e][:, slots].bitcast(FP8X4),
+                        rhs_scale=slot_plane[e][:, slots],
                         start=True,
                         stop=True,
                     )
-                nc.scalar.copy(h_bf[:, cols, :], acc[:].rearrange("p t s -> p s t"))
-            state["h_bf", e] = h_bf
+                nc.scalar.copy(rounded[e][:, slots, :], h_sums[:].rearrange("p t s -> p s t"))
 
-        def cast_wb(e):
-            wb_bf = ring.tile([P, N, PACK], BF16, name="wb_bf", align_bytes=64)
-            dst = wb_bf[:].rearrange("p (c i) j -> p c j i", i=4)
-            src = wb_raw[e][:].rearrange("p j (c i) -> p c j i", i=4)
-            if e in SCALAR_CASTS:
-                nc.scalar.copy(dst, src)
-            else:
-                nc.vector.tensor_copy(dst, src)
-            state["wb_bf", e] = wb_bf
+        def quantise(e, pieces):
+            codes = each.tile([P, C + N], U32, name="codes", align_bytes=ALIGN)
+            plane = rooms.tile([P, C + N], U8, name="plane%d" % e, align_bytes=ALIGN, offset=ROOM * (e + LAG))
+            for lo, hi in pieces:
+                nc.vector.quantize_mx(
+                    out=codes[:, lo:hi].bitcast(FP8X4),
+                    scales=plane[:, lo:hi],
+                    in_=rounded[e][:, lo:hi, :].rearrange("p c j -> p (c j)"),
+                )
+            quantised[e] = (codes, plane)
 
-        def quantise(name, e, width):
-            codes = ring.tile([P, width], U32, name=name + "_codes", align_bytes=64)
-            plane = ring.tile([P, width], U8, name=name + "_plane", align_bytes=64)
-            nc.vector.quantize_mx(
-                out=codes[:].bitcast(FP8X4),
-                scales=plane[:],
-                in_=state[name + "_bf", e][:].rearrange("p c j -> p (c j)"),
-            )
-            state[name, e] = (codes, plane)
-
-        def second_product(e):
-            xg, xs = state["x", e]
-            hq, hs = state["h", e]
-            bq, bs = state["wb", e]
-            acc = y_psum.tile([P, N // P, C], F32, name="y_acc")
+        def second_product(e, first, end, copy):
+            codes, plane = quantised[e]
+            y_sums = y_psum.tile([P, N // P, end - first], F32, name="y_sums")
             for b in range(N // P):
-                rows = slice(b * P, (b + 1) * P)
-                for u in range(C // HALF):
-                    cols = slice(u * HALF, (u + 1) * HALF)
+                wb_columns = slice(C + b * P, C + (b + 1) * P)
+                for lo in range(first, end, HALF):
+                    slots = slice(lo, lo + HALF)
+                    group = y_sums[:, b, lo - first : lo - first + HALF]
                     nc.tensor.matmul_mx(
-                        out=acc[:, b, cols],
+                        out=group,
                         lhsT=w_codes[e // SET][:, e % SET, 2 * b * P : 2 * (b + 1) * P].bitcast(FP4X4),
-                        lhsT_scale=w_plane[:, e, rows],
-                        rhs=xg[:, cols].bitcast(FP8X4),
-                        rhs_scale=xs[:, cols],
+                        lhsT_scale=w_plane[:, e, b * P : (b + 1) * P],
+                        rhs=slot_words[e][:, slots].bitcast(FP8X4),
+                        rhs_scale=slot_plane[e][:, slots],
                         start=True,
                         stop=False,
                     )
                     nc.tensor.matmul_mx(
-                        out=acc[:, b, cols],
-                        lhsT=bq[:, rows].bitcast(FP8X4),
-                        lhsT_scale=bs[:, rows],
-                        rhs=hq[:, cols].bitcast(FP8X4),
-                        rhs_scale=hs[:, cols],
+                        out=group,
+                        lhsT=codes[:, wb_columns].bitcast(FP8X4),
+                        lhsT_scale=plane[:, wb_columns],
+                        rhs=codes[:, slots].bitcast(FP8X4),
+                        rhs_scale=plane[:, slots],
                         start=False,
                         stop=True,
                     )
-            y = keep.tile([P, N // P, C], F32, name="y%d" % e)
-            nc.scalar.copy(y[:], acc[:])
-            nc.sync.dma_start(out_view[:, :, e * C : (e + 1) * C], y[:])
+            y = keep.tile([P, N // P, end - first], F32, name="y%d_%d" % (e, first))
+            copy(y[:], y_sums[:])
+            nc.sync.dma_start(out_view[:, :, e * C + first : e * C + end], y[:])
 
-        gather(0)
-        for step in range(E + 2):
+        gather(0, LEAD, E)
+        for step in range(E + LAG - 1):
             if step < E:
                 permute(step)
-                if step == 0:
-                    gather(1)
-                cast_wb(step)
+                round_wb(step)
                 first_product(step)
-            if 1 <= step <= E:
-                quantise("wb", step - 1, N)
-                quantise("h", step - 1, C)
+            if step >= LAG:
+                quantise(step - LAG, [(0, C + N)])
+                second_product(step - LAG, 0, C, nc.scalar.copy if step < E else nc.vector.tensor_copy)
             if step + LEAD < E:
-                gather(step + LEAD)
-            if step >= 2:
-                second_product(step - 2)
+                gather(step + LEAD, step + LEAD + 1, step)
+        quantise(E - 1, [(C, C + N), (0, HALF), (HALF, C)])
+        second_product(E - 1, 0, HALF, nc.scalar.copy)
+        second_product(E - 1, HALF, C, nc.vector.tensor_copy)

@@ -20,11 +20,8 @@ QUADRANT = 32
 ROWS = 4
 HALF = 128
 SET = 4
-LEAD = 3
-LAG = 2
-SCALAR_ROUNDS = 6
 H_BANKS, Y_BANKS = 6, 2
-ROOM = C + N + LEAD * C * (1 + PACK)
+ROOM = 4096
 ALIGN = 64
 
 
@@ -36,23 +33,30 @@ def tile_moe_elr_s_none_kernel(
     with ExitStack() as ctx:
         keep = ctx.enter_context(tc.tile_pool(name="keep", bufs=1))
         rooms = ctx.enter_context(tc.tile_pool(name="rooms", bufs=1))
-        each = ctx.enter_context(tc.tile_pool(name="each", bufs=E))
-        h_psum = ctx.enter_context(tc.psum_pool(name="h_psum", bufs=H_BANKS))
-        y_psum = ctx.enter_context(tc.psum_pool(name="y_psum", bufs=Y_BANKS))
+        psum = ctx.enter_context(tc.psum_pool(name="psum", bufs=8))
 
         offsets = keep.tile([P, E * C // 16], U16, name="offsets")
         x_table = keep.tile([P, T], I32, name="x_table", align_bytes=ALIGN)
-        x_rows = keep.tile([P, T // 4], I32, name="x_rows", align_bytes=ALIGN)
         x_plane = keep.tile([P, T], U8, name="x_plane", align_bytes=ALIGN)
         wa_plane_raw = [keep.tile([P, H], U8, name="wa_plane_raw%d" % s, align_bytes=ALIGN) for s in sets]
         wa_plane = [keep.tile([P, H], U8, name="wa_plane%d" % s, align_bytes=ALIGN) for s in sets]
         w_plane = keep.tile([P, E, N], U8, name="w_plane", align_bytes=ALIGN)
         w_codes = [keep.tile([P, SET, 2 * N], U8, name="w_codes%d" % s, align_bytes=ALIGN) for s in sets]
-        wa_raw = [rooms.tile([P, H], I32, name="wa_raw%d" % e, align_bytes=ALIGN, offset=ROOM * e) for e in range(E)]
         wb_raw = [keep.tile([P, PACK, N], F32, name="wb_raw%d" % e, align_bytes=ALIGN) for e in range(E)]
+        rounded = [keep.tile([P, C + N, PACK], BF16, name="rounded%d" % e, align_bytes=ALIGN) for e in range(E)]
+        wa_raw = {}
 
-        for plane in (wa_plane_raw[0], x_plane, wa_plane_raw[1], w_plane):
+        for plane in (x_plane, wa_plane_raw[0], w_plane, wa_plane_raw[1]):
             nc.vector.memset(plane[:].bitcast(I32), 0)
+
+        def load_x_plane():
+            for r in range(ROWS):
+                nc.sync.dma_start(
+                    x_plane[r:P:QUADRANT, :].bitcast(I32), x_scales[0, r : ROWS * ROWS : ROWS, :].bitcast(I32)
+                )
+
+        def load_x():
+            nc.sync.dma_start(x_table[:], x_words[0].rearrange("p t d -> p (t d)").bitcast(I32))
 
         def load_wa_plane(s):
             for q in range(ROWS):
@@ -74,67 +78,74 @@ def tile_moe_elr_s_none_kernel(
                 w_words[SET * s : SET * (s + 1), 0].rearrange("e p b -> p e b").bitcast(I32),
             )
 
-        def load_wa(e):
-            nc.sync.dma_start(wa_raw[e][:], wa_words[e, 0].rearrange("p i d -> p (i d)").bitcast(I32))
+        def load_wa(first, end):
+            wa_raw[first] = rooms.tile(
+                [P, end - first, H], I32, name="wa_raw%d" % first, align_bytes=ALIGN, offset=ROOM * first
+            )
+            nc.sync.dma_start(wa_raw[first][:], wa_words[first:end, 0].rearrange("e p i d -> p e (i d)").bitcast(I32))
 
         def load_wb(e):
             nc.sync.dma_start(wb_raw[e][:], wb[e].rearrange("(p j) n -> p j n", j=PACK))
 
-        for r in range(ROWS):
-            nc.sync.dma_start(x_rows[r:P:QUADRANT, :], x_scales[0, r : ROWS * ROWS : ROWS, :].bitcast(I32))
         nc.sync.dma_start(offsets[:], offs)
-        nc.sync.dma_start(x_table[:], x_words[0].rearrange("p t d -> p (t d)").bitcast(I32))
-        for e in range(LAG):
-            load_wb(e)
+        load_x()
+        load_x_plane()
+        load_wb(0)
+        load_wb(1)
         load_wa_plane(0)
-        for e in range(E):
-            load_wa(e)
-            if e == LAG:
-                load_w_plane()
-            if e % SET == LAG:
-                load_w(e // SET)
-            if e + 1 == SET:
-                load_wa_plane(1)
-            if e + LAG < SCALAR_ROUNDS:
-                load_wb(e + LAG)
-        for e in range(SCALAR_ROUNDS, E):
-            load_wb(e)
-
-        for q in range(ROWS):
-            live = slice(QUADRANT * q, QUADRANT * q + ROWS)
-            nc.vector.tensor_copy(x_plane[live, :].bitcast(I32), x_rows[live, :])
+        load_wb(2)
+        load_wa(0, 1)
+        load_wb(3)
+        load_wa(1, 3)
+        load_wa(3, 4)
+        load_w_plane()
+        load_w(0)
+        load_wb(4)
+        load_wa_plane(1)
+        load_wa(4, 6)
+        load_wa(6, 8)
+        load_w(1)
+        load_wb(5)
+        load_wb(6)
+        load_wb(7)
 
         out_view = out.rearrange("(b p) s -> p b s", p=P)
-        slot_words, slot_plane, wa_codes, rounded, quantised = {}, {}, {}, {}, {}
+        slot_words, slot_plane, wa_codes, quantised = {}, {}, {}, {}
 
-        def gather(first, end, room):
-            width = (end - first) * C
-            place = ROOM * room + C + N
-            scale_bytes = rooms.tile([P, width], U8, name="slot_plane%d" % first, align_bytes=ALIGN, offset=place)
-            words = rooms.tile([P, width], U32, name="slot_words%d" % first, align_bytes=ALIGN, offset=place + width)
+        def gather_words(first, end, room):
+            words = rooms.tile(
+                [P, (end - first) * C], U32, name="slot_words%d" % first, align_bytes=ALIGN, offset=ROOM * room
+            )
             entries = offsets[:, first * C // 16 : end * C // 16]
             nc.vector.tensor_copy(words[:], x_table[:].bitcast(U32).indirect(entries))
+            for e in range(first, end):
+                slot_words[e] = words[:, (e - first) * C : (e - first + 1) * C]
+
+        def gather_bytes(first, end, room):
+            scale_bytes = rooms.tile(
+                [P, (end - first) * C], U8, name="slot_plane%d" % first, align_bytes=ALIGN, offset=ROOM * room
+            )
+            entries = offsets[:, first * C // 16 : end * C // 16]
             nc.vector.tensor_copy(scale_bytes[:], x_plane[:].indirect(entries))
             for e in range(first, end):
-                own = slice((e - first) * C, (e - first + 1) * C)
-                slot_words[e] = words[:, own]
-                slot_plane[e] = scale_bytes[:, own]
+                slot_plane[e] = scale_bytes[:, (e - first) * C : (e - first + 1) * C]
 
-        def permute(e):
-            if e % SET == 0:
-                nc.vector.tensor_copy(
-                    wa_plane[e // SET][:].rearrange("p (t c i) -> p c t i", t=PACK, i=16),
-                    wa_plane_raw[e // SET][:].rearrange("p (c i t) -> p c t i", t=PACK, i=16),
-                )
-            wa_codes[e] = each.tile([P, H], I32, name="wa_codes", align_bytes=ALIGN)
+        def permute_plane(s):
             nc.vector.tensor_copy(
-                wa_codes[e][:].rearrange("p (t c i) -> p c t i", t=PACK, i=4),
-                wa_raw[e][:].rearrange("p (c i t) -> p c t i", t=PACK, i=4),
+                wa_plane[s][:].rearrange("p (t c i) -> p c t i", t=PACK, i=16),
+                wa_plane_raw[s][:].rearrange("p (c i t) -> p c t i", t=PACK, i=16),
             )
 
-        def round_wb(e):
-            rounded[e] = each.tile([P, C + N, PACK], BF16, name="rounded", align_bytes=ALIGN)
-            copy = nc.scalar.copy if e < SCALAR_ROUNDS else nc.vector.tensor_copy
+        def permute(first, end):
+            codes = keep.tile([P, end - first, H], I32, name="wa_codes%d" % first, align_bytes=ALIGN)
+            nc.vector.tensor_copy(
+                codes[:].rearrange("p e (t c i) -> p e c t i", t=PACK, i=4),
+                wa_raw[first][:].rearrange("p e (c i t) -> p e c t i", t=PACK, i=4),
+            )
+            for e in range(first, end):
+                wa_codes[e] = codes[:, e - first, :]
+
+        def round_wb(e, copy):
             copy(
                 rounded[e][:, C:, :].rearrange("p (c i) j -> p c j i", i=4),
                 wb_raw[e][:].rearrange("p j (c i) -> p c j i", i=4),
@@ -144,7 +155,7 @@ def tile_moe_elr_s_none_kernel(
             first_row = ROWS * (e % SET)
             for lo in range(0, C, HALF):
                 slots = slice(lo, lo + HALF)
-                h_sums = h_psum.tile([P, PACK, HALF], F32, name="h_sums")
+                h_sums = psum.tile([P, PACK, HALF], F32, name="sums")
                 for t in range(PACK):
                     columns = slice(t * P, (t + 1) * P)
                     nc.tensor.matmul_mx(
@@ -158,9 +169,9 @@ def tile_moe_elr_s_none_kernel(
                     )
                 nc.scalar.copy(rounded[e][:, slots, :], h_sums[:].rearrange("p t s -> p s t"))
 
-        def quantise(e, pieces):
-            codes = each.tile([P, C + N], U32, name="codes", align_bytes=ALIGN)
-            plane = rooms.tile([P, C + N], U8, name="plane%d" % e, align_bytes=ALIGN, offset=ROOM * (e + LAG))
+        def quantise(e, pieces, place):
+            codes = keep.tile([P, C + N], U32, name="codes%d" % e, align_bytes=ALIGN)
+            plane = rooms.tile([P, C + N], U8, name="plane%d" % e, align_bytes=ALIGN, offset=place)
             for lo, hi in pieces:
                 nc.vector.quantize_mx(
                     out=codes[:, lo:hi].bitcast(FP8X4),
@@ -171,7 +182,7 @@ def tile_moe_elr_s_none_kernel(
 
         def second_product(e, first, end, copy):
             codes, plane = quantised[e]
-            y_sums = y_psum.tile([P, N // P, end - first], F32, name="y_sums")
+            y_sums = psum.tile([P, N // P, end - first], F32, name="sums")
             for b in range(N // P):
                 wb_columns = slice(C + b * P, C + (b + 1) * P)
                 for lo in range(first, end, HALF):
@@ -199,17 +210,51 @@ def tile_moe_elr_s_none_kernel(
             copy(y[:], y_sums[:])
             nc.sync.dma_start(out_view[:, :, e * C + first : e * C + end], y[:])
 
-        gather(0, LEAD, E)
-        for step in range(E + LAG - 1):
-            if step < E:
-                permute(step)
-                round_wb(step)
-                first_product(step)
-            if step >= LAG:
-                quantise(step - LAG, [(0, C + N)])
-                second_product(step - LAG, 0, C, nc.scalar.copy if step < E else nc.vector.tensor_copy)
-            if step + LEAD < E:
-                gather(step + LEAD, step + LEAD + 1, step)
-        quantise(E - 1, [(C, C + N), (0, HALF), (HALF, C)])
-        second_product(E - 1, 0, HALF, nc.scalar.copy)
-        second_product(E - 1, HALF, C, nc.vector.tensor_copy)
+        on_scalar, on_vector = nc.scalar.copy, nc.vector.tensor_copy
+        whole = [(0, C + N)]
+        gather_words(0, 3, 9)
+        gather_bytes(0, 3, 8)
+        permute_plane(0)
+        permute(0, 1)
+        round_wb(0, on_scalar)
+        round_wb(1, on_scalar)
+        round_wb(2, on_scalar)
+        first_product(0)
+        round_wb(3, on_scalar)
+        gather_bytes(3, 6, 0)
+        permute(1, 3)
+        first_product(1)
+        first_product(2)
+        gather_words(3, 6, 1)
+        permute(3, 4)
+        first_product(3)
+        quantise(0, whole, ROOM * 10 + 0)
+        second_product(0, 0, C, on_scalar)
+        gather_bytes(6, 8, 3)
+        round_wb(4, on_scalar)
+        permute_plane(1)
+        permute(4, 6)
+        first_product(4)
+        first_product(5)
+        gather_words(6, 8, 4)
+        quantise(1, whole, ROOM * 4 + 3072 + 512)
+        second_product(1, 0, C, on_scalar)
+        permute(6, 8)
+        first_product(6)
+        first_product(7)
+        quantise(2, whole, ROOM * 6 + 3072 + 0)
+        second_product(2, 0, C, on_scalar)
+        quantise(3, whole, ROOM * 6 + 3072 + 512)
+        second_product(3, 0, C, on_scalar)
+        round_wb(5, on_vector)
+        quantise(4, whole, ROOM * 10 + 2048)
+        second_product(4, 0, C, on_scalar)
+        round_wb(6, on_vector)
+        quantise(5, whole, ROOM * 10 + 2560)
+        second_product(5, 0, C, on_scalar)
+        round_wb(7, on_vector)
+        quantise(6, whole, ROOM * 10 + 3072)
+        second_product(6, 0, C, on_scalar)
+        quantise(7, [(C, C + N), (0, HALF), (HALF, C)], ROOM * 10 + 3584)
+        second_product(7, 0, HALF, on_scalar)
+        second_product(7, HALF, C, on_vector)

@@ -42,7 +42,7 @@ def tile_moe_elr_s_none_kernel(
         wa_plane = [keep.tile([P, H], U8, name="wa_plane%d" % s, align_bytes=ALIGN) for s in sets]
         w_plane = keep.tile([P, E, N], U8, name="w_plane", align_bytes=ALIGN)
         w_codes = [keep.tile([P, SET, 2 * N], U8, name="w_codes%d" % s, align_bytes=ALIGN) for s in sets]
-        wb_raw = [keep.tile([P, PACK, N], F32, name="wb_raw%d" % e, align_bytes=ALIGN) for e in range(E)]
+        wb_raw = {}
         rounded = [keep.tile([P, C + N, PACK], BF16, name="rounded%d" % e, align_bytes=ALIGN) for e in range(E)]
         wa_raw = {}
 
@@ -55,8 +55,8 @@ def tile_moe_elr_s_none_kernel(
                     x_plane[r:P:QUADRANT, :].bitcast(I32), x_scales[0, r : ROWS * ROWS : ROWS, :].bitcast(I32)
                 )
 
-        def load_x():
-            nc.sync.dma_start(x_table[:], x_words[0].rearrange("p t d -> p (t d)").bitcast(I32))
+        def load_x(lo, hi):
+            nc.sync.dma_start(x_table[:, lo:hi], x_words[0, :, lo:hi, :].rearrange("p t d -> p (t d)").bitcast(I32))
 
         def load_wa_plane(s):
             for q in range(ROWS):
@@ -84,37 +84,43 @@ def tile_moe_elr_s_none_kernel(
             )
             nc.sync.dma_start(wa_raw[first][:], wa_words[first:end, 0].rearrange("e p i d -> p e (i d)").bitcast(I32))
 
-        def load_wb(e):
-            nc.sync.dma_start(wb_raw[e][:], wb[e].rearrange("(p j) n -> p j n", j=PACK))
+        def load_wb(first, end):
+            tile = rooms.tile(
+                [P, end - first, PACK * N], F32, name="wb_raw%d" % first, align_bytes=ALIGN, offset=ROOM * (20 + first)
+            )
+            nc.sync.dma_start(tile[:], wb[first:end].rearrange("e (p j) n -> p e (j n)", j=PACK))
+            for e in range(first, end):
+                wb_raw[e] = tile[:, e - first, :]
 
         nc.sync.dma_start(offsets[:], offs)
-        load_x()
+        load_x(0, T)
         load_x_plane()
-        load_wb(0)
-        load_wb(1)
+        load_wb(0, 1)
+        load_wb(1, 2)
         load_wa_plane(0)
-        load_wb(2)
+        load_wb(2, 3)
         load_wa(0, 1)
-        load_wb(3)
+        load_wb(3, 4)
         load_wa(1, 3)
         load_wa(3, 4)
         load_w_plane()
         load_w(0)
-        load_wb(4)
+        load_wb(4, 5)
         load_wa_plane(1)
-        load_wa(4, 6)
-        load_wa(6, 8)
+        load_wa(4, 5)
+        load_wa(5, 6)
+        load_wa(6, 7)
         load_w(1)
-        load_wb(5)
-        load_wb(6)
-        load_wb(7)
+        load_wb(5, 7)
+        load_wa(7, 8)
+        load_wb(7, 8)
 
         out_view = out.rearrange("(b p) s -> p b s", p=P)
         slot_words, slot_plane, wa_codes, quantised = {}, {}, {}, {}
 
         def gather_words(first, end, room):
             words = rooms.tile(
-                [P, (end - first) * C], U32, name="slot_words%d" % first, align_bytes=ALIGN, offset=ROOM * room
+                [P, (end - first) * C], U32, name="slot_words%d" % first, align_bytes=ALIGN, offset=ROOM * room + 1024
             )
             entries = offsets[:, first * C // 16 : end * C // 16]
             nc.vector.tensor_copy(words[:], x_table[:].bitcast(U32).indirect(entries))
@@ -137,18 +143,18 @@ def tile_moe_elr_s_none_kernel(
             )
 
         def permute(first, end):
-            codes = keep.tile([P, end - first, H], I32, name="wa_codes%d" % first, align_bytes=ALIGN)
+            codes = keep.tile([P, PACK, end - first, P], I32, name="wa_codes%d" % first, align_bytes=ALIGN)
             nc.vector.tensor_copy(
-                codes[:].rearrange("p e (t c i) -> p e c t i", t=PACK, i=4),
-                wa_raw[first][:].rearrange("p e (c i t) -> p e c t i", t=PACK, i=4),
+                codes[:].rearrange("p t e (c i) -> p (e c) t i", i=4),
+                wa_raw[first][:].rearrange("p e (c i t) -> p (e c) t i", t=PACK, i=4),
             )
             for e in range(first, end):
-                wa_codes[e] = codes[:, e - first, :]
+                wa_codes[e] = codes[:, :, e - first, :]
 
         def round_wb(e, copy):
             copy(
                 rounded[e][:, C:, :].rearrange("p (c i) j -> p c j i", i=4),
-                wb_raw[e][:].rearrange("p j (c i) -> p c j i", i=4),
+                wb_raw[e].rearrange("p (j c i) -> p c j i", j=PACK, i=4),
             )
 
         def first_product(e):
@@ -160,7 +166,7 @@ def tile_moe_elr_s_none_kernel(
                     columns = slice(t * P, (t + 1) * P)
                     nc.tensor.matmul_mx(
                         out=h_sums[:, t, :],
-                        lhsT=wa_codes[e][:, columns].bitcast(FP8X4),
+                        lhsT=wa_codes[e][:, t, :].bitcast(FP8X4),
                         lhsT_scale=wa_plane[e // SET][first_row:P, columns],
                         rhs=slot_words[e][:, slots].bitcast(FP8X4),
                         rhs_scale=slot_plane[e][:, slots],
@@ -180,7 +186,9 @@ def tile_moe_elr_s_none_kernel(
                 )
             quantised[e] = (codes, plane)
 
-        def second_product(e, first, end, copy):
+        staged = {}
+
+        def second_product(e, first, end, copy, group_first, group_end):
             codes, plane = quantised[e]
             y_sums = psum.tile([P, N // P, end - first], F32, name="sums")
             for b in range(N // P):
@@ -206,9 +214,15 @@ def tile_moe_elr_s_none_kernel(
                         start=False,
                         stop=True,
                     )
-            y = keep.tile([P, N // P, end - first], F32, name="y%d_%d" % (e, first))
-            copy(y[:], y_sums[:])
-            nc.sync.dma_start(out_view[:, :, e * C + first : e * C + end], y[:])
+            if group_first not in staged:
+                staged[group_first] = rooms.tile(
+                    [P, N // P, group_end - group_first], F32, name="y%d" % group_first,
+                    offset=ROOM * 27 if e == 6 else ROOM * 28 + 8 * group_first,
+                )
+            y = staged[group_first]
+            copy(y[:, :, e * C + first - group_first : e * C + end - group_first], y_sums[:])
+            if e * C + end == group_end:
+                nc.sync.dma_start(out_view[:, :, group_first:group_end], y[:])
 
         on_scalar, on_vector = nc.scalar.copy, nc.vector.tensor_copy
         whole = [(0, C + N)]
@@ -226,35 +240,37 @@ def tile_moe_elr_s_none_kernel(
         first_product(1)
         first_product(2)
         gather_words(3, 6, 1)
+        quantise(0, whole, ROOM * 1 + 0)
+        second_product(0, 0, C, on_scalar, 0 * C, 2 * C)
         permute(3, 4)
         first_product(3)
-        quantise(0, whole, ROOM * 10 + 0)
-        second_product(0, 0, C, on_scalar)
-        gather_bytes(6, 8, 3)
+        quantise(1, whole, ROOM * 10 + 512)
+        second_product(1, 0, C, on_scalar, 0 * C, 2 * C)
         round_wb(4, on_scalar)
         permute_plane(1)
-        permute(4, 6)
+        permute(4, 5)
         first_product(4)
-        first_product(5)
         gather_words(6, 8, 4)
-        quantise(1, whole, ROOM * 4 + 3072 + 512)
-        second_product(1, 0, C, on_scalar)
-        permute(6, 8)
+        quantise(2, whole, ROOM * 4 + 0)
+        second_product(2, 0, C, on_scalar, 2 * C, 3 * C)
+        permute(5, 6)
+        first_product(5)
+        gather_bytes(6, 8, 5)
+        quantise(3, whole, ROOM * 5 + 1024)
+        second_product(3, 0, C, on_scalar, 3 * C, 4 * C)
+        permute(6, 7)
         first_product(6)
-        first_product(7)
-        quantise(2, whole, ROOM * 6 + 3072 + 0)
-        second_product(2, 0, C, on_scalar)
-        quantise(3, whole, ROOM * 6 + 3072 + 512)
-        second_product(3, 0, C, on_scalar)
-        round_wb(5, on_vector)
         quantise(4, whole, ROOM * 10 + 2048)
-        second_product(4, 0, C, on_scalar)
+        second_product(4, 0, C, on_scalar, 4 * C, 5 * C)
+        round_wb(5, on_vector)
         round_wb(6, on_vector)
         quantise(5, whole, ROOM * 10 + 2560)
-        second_product(5, 0, C, on_scalar)
-        round_wb(7, on_vector)
+        second_product(5, 0, C, on_scalar, 5 * C, 6 * C)
+        permute(7, 8)
+        first_product(7)
         quantise(6, whole, ROOM * 10 + 3072)
-        second_product(6, 0, C, on_scalar)
+        round_wb(7, on_vector)
+        second_product(6, 0, C, on_vector, 6 * C, 7 * C)
         quantise(7, [(C, C + N), (0, HALF), (HALF, C)], ROOM * 10 + 3584)
-        second_product(7, 0, HALF, on_scalar)
-        second_product(7, HALF, C, on_vector)
+        second_product(7, 0, HALF, on_scalar, 7 * C, 7 * C + HALF)
+        second_product(7, HALF, C, on_vector, 7 * C + HALF, 8 * C)

@@ -241,31 +241,31 @@ def tile_moe_elr_s_none_kernel(
         first_product(2)
         gather_words(3, 6, 1)
         quantise(0, whole, ROOM * 1 + 0)
-        second_product(0, 0, C, on_scalar, 0 * C, 2 * C)
+        second_product(0, 0, C, on_scalar, 0 * C, 4 * C)
         permute(3, 4)
         first_product(3)
         quantise(1, whole, ROOM * 10 + 512)
-        second_product(1, 0, C, on_scalar, 0 * C, 2 * C)
+        second_product(1, 0, C, on_scalar, 0 * C, 4 * C)
         round_wb(4, on_scalar)
         permute_plane(1)
         permute(4, 5)
         first_product(4)
         gather_words(6, 8, 4)
         quantise(2, whole, ROOM * 4 + 0)
-        second_product(2, 0, C, on_scalar, 2 * C, 3 * C)
+        second_product(2, 0, C, on_scalar, 0 * C, 4 * C)
         permute(5, 6)
         first_product(5)
         gather_bytes(6, 8, 5)
         quantise(3, whole, ROOM * 5 + 1024)
-        second_product(3, 0, C, on_scalar, 3 * C, 4 * C)
+        second_product(3, 0, C, on_scalar, 0 * C, 4 * C)
         permute(6, 7)
         first_product(6)
         quantise(4, whole, ROOM * 10 + 2048)
-        second_product(4, 0, C, on_scalar, 4 * C, 5 * C)
+        second_product(4, 0, C, on_scalar, 4 * C, 6 * C)
         round_wb(5, on_vector)
         round_wb(6, on_vector)
         quantise(5, whole, ROOM * 10 + 2560)
-        second_product(5, 0, C, on_scalar, 5 * C, 6 * C)
+        second_product(5, 0, C, on_scalar, 4 * C, 6 * C)
         permute(7, 8)
         first_product(7)
         quantise(6, whole, ROOM * 10 + 3072)

@@ -38,7 +38,9 @@ def tile_moe_elr_s_none_kernel(
         offsets = keep.tile([P, E * C // 16], U16, name="offsets")
         x_table = keep.tile([P, T], I32, name="x_table", align_bytes=ALIGN)
         x_plane = keep.tile([P, T], U8, name="x_plane", align_bytes=ALIGN)
-        wa_plane_raw = [keep.tile([P, H], U8, name="wa_plane_raw%d" % s, align_bytes=ALIGN) for s in sets]
+        wa_plane_raw = [
+            rooms.tile([P, H], U8, name="wa_plane_raw%d" % s, align_bytes=ALIGN, offset=ROOM * (11 + s)) for s in sets
+        ]
         wa_plane = [keep.tile([P, H], U8, name="wa_plane%d" % s, align_bytes=ALIGN) for s in sets]
         w_plane = keep.tile([P, E, N], U8, name="w_plane", align_bytes=ALIGN)
         w_codes = [keep.tile([P, SET, 2 * N], U8, name="w_codes%d" % s, align_bytes=ALIGN) for s in sets]
@@ -97,19 +99,17 @@ def tile_moe_elr_s_none_kernel(
         load_x_plane()
         load_wb(0, 1)
         load_wb(1, 2)
-        load_wa_plane(0)
         load_wb(2, 3)
         load_wa(0, 1)
+        load_wa_plane(0)
         load_wb(3, 4)
         load_wa(1, 3)
-        load_wa(3, 4)
-        load_w_plane()
-        load_w(0)
         load_wb(4, 5)
+        load_wa(3, 4)
         load_wa_plane(1)
-        load_wa(4, 5)
-        load_wa(5, 6)
-        load_wa(6, 7)
+        load_wa(4, 7)
+        load_w(0)
+        load_w_plane()
         load_w(1)
         load_wb(5, 7)
         load_wa(7, 8)
@@ -217,7 +217,7 @@ def tile_moe_elr_s_none_kernel(
             if group_first not in staged:
                 staged[group_first] = rooms.tile(
                     [P, N // P, group_end - group_first], F32, name="y%d" % group_first,
-                    offset=ROOM * 27 if e == 6 else ROOM * 28 + 8 * group_first,
+                    offset=ROOM * 27 if e == 99 else ROOM * 28 + 8 * group_first,
                 )
             y = staged[group_first]
             copy(y[:, :, e * C + first - group_first : e * C + end - group_first], y_sums[:])
@@ -228,49 +228,47 @@ def tile_moe_elr_s_none_kernel(
         whole = [(0, C + N)]
         gather_words(0, 3, 9)
         gather_bytes(0, 3, 8)
-        permute_plane(0)
         permute(0, 1)
+        permute_plane(0)
         round_wb(0, on_scalar)
         round_wb(1, on_scalar)
         round_wb(2, on_scalar)
         first_product(0)
         round_wb(3, on_scalar)
-        gather_bytes(3, 6, 0)
+        gather_bytes(3, 6, 11)
         permute(1, 3)
         first_product(1)
         first_product(2)
+        round_wb(4, on_scalar)
         gather_words(3, 6, 1)
         quantise(0, whole, ROOM * 1 + 0)
-        second_product(0, 0, C, on_scalar, 0 * C, 4 * C)
         permute(3, 4)
         first_product(3)
         quantise(1, whole, ROOM * 10 + 512)
-        second_product(1, 0, C, on_scalar, 0 * C, 4 * C)
-        round_wb(4, on_scalar)
         permute_plane(1)
-        permute(4, 5)
+        permute(4, 7)
         first_product(4)
+        second_product(0, 0, C, on_scalar, 0 * C, 3 * C)
+        second_product(1, 0, C, on_scalar, 0 * C, 3 * C)
         gather_words(6, 8, 4)
-        quantise(2, whole, ROOM * 4 + 0)
-        second_product(2, 0, C, on_scalar, 0 * C, 4 * C)
-        permute(5, 6)
+        quantise(2, whole, ROOM * 4 + 512)
         first_product(5)
-        gather_bytes(6, 8, 5)
-        quantise(3, whole, ROOM * 5 + 1024)
-        second_product(3, 0, C, on_scalar, 0 * C, 4 * C)
-        permute(6, 7)
+        second_product(2, 0, C, on_scalar, 0 * C, 3 * C)
+        gather_bytes(6, 8, 4)
+        quantise(3, whole, ROOM * 4 + 3072)
+        second_product(3, 0, C, on_scalar, 3 * C, 5 * C)
         first_product(6)
         quantise(4, whole, ROOM * 10 + 2048)
-        second_product(4, 0, C, on_scalar, 4 * C, 6 * C)
+        second_product(4, 0, C, on_scalar, 3 * C, 5 * C)
         round_wb(5, on_vector)
         round_wb(6, on_vector)
-        quantise(5, whole, ROOM * 10 + 2560)
-        second_product(5, 0, C, on_scalar, 4 * C, 6 * C)
         permute(7, 8)
         first_product(7)
+        quantise(5, whole, ROOM * 10 + 2560)
+        second_product(5, 0, C, on_scalar, 5 * C, 6 * C)
         quantise(6, whole, ROOM * 10 + 3072)
+        second_product(6, 0, C, on_scalar, 6 * C, 7 * C)
         round_wb(7, on_vector)
-        second_product(6, 0, C, on_vector, 6 * C, 7 * C)
         quantise(7, [(C, C + N), (0, HALF), (HALF, C)], ROOM * 10 + 3584)
         second_product(7, 0, HALF, on_scalar, 7 * C, 7 * C + HALF)
         second_product(7, HALF, C, on_vector, 7 * C + HALF, 8 * C)

@@ -20,9 +20,18 @@ QUADRANT = 32
 ROWS = 4
 HALF = 128
 SET = 4
-H_BANKS, Y_BANKS = 6, 2
-ROOM = 4096
+BANKS = 8
 ALIGN = 64
+
+ROOM = 4096
+FIRST_BYTES_ROOM, FIRST_WORDS_ROOM = 8, 9
+PLANES_ROOM = 10
+RAW_PLANE_ROOM = 11
+WB_ROOM = 20
+Y_ROOM = 28
+PLANE = C + N
+WORDS_AT = 1024
+BEHIND_WORDS = WORDS_AT + 2 * C * PACK
 
 
 def tile_moe_elr_s_none_kernel(
@@ -33,20 +42,20 @@ def tile_moe_elr_s_none_kernel(
     with ExitStack() as ctx:
         keep = ctx.enter_context(tc.tile_pool(name="keep", bufs=1))
         rooms = ctx.enter_context(tc.tile_pool(name="rooms", bufs=1))
-        psum = ctx.enter_context(tc.psum_pool(name="psum", bufs=8))
+        psum = ctx.enter_context(tc.psum_pool(name="psum", bufs=BANKS))
 
         offsets = keep.tile([P, E * C // 16], U16, name="offsets")
         x_table = keep.tile([P, T], I32, name="x_table", align_bytes=ALIGN)
         x_plane = keep.tile([P, T], U8, name="x_plane", align_bytes=ALIGN)
         wa_plane_raw = [
-            rooms.tile([P, H], U8, name="wa_plane_raw%d" % s, align_bytes=ALIGN, offset=ROOM * (11 + s)) for s in sets
+            rooms.tile([P, H], U8, name="wa_plane_raw%d" % s, align_bytes=ALIGN, offset=ROOM * (RAW_PLANE_ROOM + s))
+            for s in sets
         ]
         wa_plane = [keep.tile([P, H], U8, name="wa_plane%d" % s, align_bytes=ALIGN) for s in sets]
         w_plane = keep.tile([P, E, N], U8, name="w_plane", align_bytes=ALIGN)
         w_codes = [keep.tile([P, SET, 2 * N], U8, name="w_codes%d" % s, align_bytes=ALIGN) for s in sets]
-        wb_raw = {}
         rounded = [keep.tile([P, C + N, PACK], BF16, name="rounded%d" % e, align_bytes=ALIGN) for e in range(E)]
-        wa_raw = {}
+        wa_raw, wb_raw = {}, {}
 
         for plane in (x_plane, wa_plane_raw[0], w_plane, wa_plane_raw[1]):
             nc.vector.memset(plane[:].bitcast(I32), 0)
@@ -56,9 +65,6 @@ def tile_moe_elr_s_none_kernel(
                 nc.sync.dma_start(
                     x_plane[r:P:QUADRANT, :].bitcast(I32), x_scales[0, r : ROWS * ROWS : ROWS, :].bitcast(I32)
                 )
-
-        def load_x(lo, hi):
-            nc.sync.dma_start(x_table[:, lo:hi], x_words[0, :, lo:hi, :].rearrange("p t d -> p (t d)").bitcast(I32))
 
         def load_wa_plane(s):
             for q in range(ROWS):
@@ -87,19 +93,17 @@ def tile_moe_elr_s_none_kernel(
             nc.sync.dma_start(wa_raw[first][:], wa_words[first:end, 0].rearrange("e p i d -> p e (i d)").bitcast(I32))
 
         def load_wb(first, end):
-            tile = rooms.tile(
-                [P, end - first, PACK * N], F32, name="wb_raw%d" % first, align_bytes=ALIGN, offset=ROOM * (20 + first)
-            )
-            nc.sync.dma_start(tile[:], wb[first:end].rearrange("e (p j) n -> p e (j n)", j=PACK))
+            place = ROOM * (WB_ROOM + first)
+            rows = rooms.tile([P, end - first, PACK * N], F32, name="wb_raw%d" % first, align_bytes=ALIGN, offset=place)
+            nc.sync.dma_start(rows[:], wb[first:end].rearrange("e (p j) n -> p e (j n)", j=PACK))
             for e in range(first, end):
-                wb_raw[e] = tile[:, e - first, :]
+                wb_raw[e] = rows[:, e - first, :]
 
         nc.sync.dma_start(offsets[:], offs)
-        load_x(0, T)
+        nc.sync.dma_start(x_table[:], x_words[0].rearrange("p t d -> p (t d)").bitcast(I32))
         load_x_plane()
-        load_wb(0, 1)
-        load_wb(1, 2)
-        load_wb(2, 3)
+        for e in range(3):
+            load_wb(e, e + 1)
         load_wa(0, 1)
         load_wa_plane(0)
         load_wb(3, 4)
@@ -116,12 +120,11 @@ def tile_moe_elr_s_none_kernel(
         load_wb(7, 8)
 
         out_view = out.rearrange("(b p) s -> p b s", p=P)
-        slot_words, slot_plane, wa_codes, quantised = {}, {}, {}, {}
+        slot_words, slot_plane, wa_codes, quantised, staged = {}, {}, {}, {}, {}
 
         def gather_words(first, end, room):
-            words = rooms.tile(
-                [P, (end - first) * C], U32, name="slot_words%d" % first, align_bytes=ALIGN, offset=ROOM * room + 1024
-            )
+            place = ROOM * room + WORDS_AT
+            words = rooms.tile([P, (end - first) * C], U32, name="slot_words%d" % first, align_bytes=ALIGN, offset=place)
             entries = offsets[:, first * C // 16 : end * C // 16]
             nc.vector.tensor_copy(words[:], x_table[:].bitcast(U32).indirect(entries))
             for e in range(first, end):
@@ -136,25 +139,25 @@ def tile_moe_elr_s_none_kernel(
             for e in range(first, end):
                 slot_plane[e] = scale_bytes[:, (e - first) * C : (e - first + 1) * C]
 
+        def permute(first, end):
+            codes = keep.tile([P, PACK, end - first, P], I32, name="wa_codes%d" % first, align_bytes=ALIGN)
+            nc.vector.tensor_copy(
+                codes[:].rearrange("p (u v) e (c i) -> p (e c) u i v", v=2, i=4),
+                wa_raw[first][:].rearrange("p e (c i u v) -> p (e c) u i v", u=2, v=2, i=4),
+            )
+            for e in range(first, end):
+                wa_codes[e] = codes[:, :, e - first, :]
+
         def permute_plane(s):
             nc.vector.tensor_copy(
                 wa_plane[s][:].rearrange("p (t c i) -> p c t i", t=PACK, i=16),
                 wa_plane_raw[s][:].rearrange("p (c i t) -> p c t i", t=PACK, i=16),
             )
 
-        def permute(first, end):
-            codes = keep.tile([P, PACK, end - first, P], I32, name="wa_codes%d" % first, align_bytes=ALIGN)
-            nc.vector.tensor_copy(
-                codes[:].rearrange("p t e (c i) -> p (e c) t i", i=4),
-                wa_raw[first][:].rearrange("p e (c i t) -> p (e c) t i", t=PACK, i=4),
-            )
-            for e in range(first, end):
-                wa_codes[e] = codes[:, :, e - first, :]
-
         def round_wb(e, copy):
             copy(
-                rounded[e][:, C:, :].rearrange("p (c i) j -> p c j i", i=4),
-                wb_raw[e].rearrange("p (j c i) -> p c j i", j=PACK, i=4),
+                rounded[e][:, C:, :].rearrange("p (c i) j -> p c j i", i=2),
+                wb_raw[e].rearrange("p (j c i) -> p c j i", j=PACK, i=2),
             )
 
         def first_product(e):
@@ -163,11 +166,10 @@ def tile_moe_elr_s_none_kernel(
                 slots = slice(lo, lo + HALF)
                 h_sums = psum.tile([P, PACK, HALF], F32, name="sums")
                 for t in range(PACK):
-                    columns = slice(t * P, (t + 1) * P)
                     nc.tensor.matmul_mx(
                         out=h_sums[:, t, :],
                         lhsT=wa_codes[e][:, t, :].bitcast(FP8X4),
-                        lhsT_scale=wa_plane[e // SET][first_row:P, columns],
+                        lhsT_scale=wa_plane[e // SET][first_row:P, t * P : (t + 1) * P],
                         rhs=slot_words[e][:, slots].bitcast(FP8X4),
                         rhs_scale=slot_plane[e][:, slots],
                         start=True,
@@ -177,7 +179,7 @@ def tile_moe_elr_s_none_kernel(
 
         def quantise(e, pieces, place):
             codes = keep.tile([P, C + N], U32, name="codes%d" % e, align_bytes=ALIGN)
-            plane = rooms.tile([P, C + N], U8, name="plane%d" % e, align_bytes=ALIGN, offset=place)
+            plane = rooms.tile([P, PLANE], U8, name="plane%d" % e, align_bytes=ALIGN, offset=place)
             for lo, hi in pieces:
                 nc.vector.quantize_mx(
                     out=codes[:, lo:hi].bitcast(FP8X4),
@@ -186,15 +188,14 @@ def tile_moe_elr_s_none_kernel(
                 )
             quantised[e] = (codes, plane)
 
-        staged = {}
-
-        def second_product(e, first, end, copy, group_first, group_end):
+        def second_product(first, end, copy, store_first, store_end):
+            e = first // C
             codes, plane = quantised[e]
             y_sums = psum.tile([P, N // P, end - first], F32, name="sums")
             for b in range(N // P):
                 wb_columns = slice(C + b * P, C + (b + 1) * P)
                 for lo in range(first, end, HALF):
-                    slots = slice(lo, lo + HALF)
+                    slots = slice(lo - e * C, lo - e * C + HALF)
                     group = y_sums[:, b, lo - first : lo - first + HALF]
                     nc.tensor.matmul_mx(
                         out=group,
@@ -214,61 +215,72 @@ def tile_moe_elr_s_none_kernel(
                         start=False,
                         stop=True,
                     )
-            if group_first not in staged:
-                staged[group_first] = rooms.tile(
-                    [P, N // P, group_end - group_first], F32, name="y%d" % group_first,
-                    offset=ROOM * 27 if e == 99 else ROOM * 28 + 8 * group_first,
+            if first == store_first:
+                place = ROOM * Y_ROOM + 4 * (N // P) * store_first
+                staged[store_first] = rooms.tile(
+                    [P, N // P, store_end - store_first], F32, name="y%d" % store_first, offset=place
                 )
-            y = staged[group_first]
-            copy(y[:, :, e * C + first - group_first : e * C + end - group_first], y_sums[:])
-            if e * C + end == group_end:
-                nc.sync.dma_start(out_view[:, :, group_first:group_end], y[:])
+            y = staged[store_first]
+            copy(y[:, :, first - store_first : end - store_first], y_sums[:])
+            if end == store_end:
+                nc.sync.dma_start(out_view[:, :, store_first:store_end], y[:])
+
+        def whole_y(e, copy, store_first, store_end):
+            second_product(e * C, (e + 1) * C, copy, store_first * C, store_end * C)
+
+        def own_place(e):
+            return ROOM * PLANES_ROOM + PLANE * e
 
         on_scalar, on_vector = nc.scalar.copy, nc.vector.tensor_copy
         whole = [(0, C + N)]
-        gather_words(0, 3, 9)
-        gather_bytes(0, 3, 8)
+
+        gather_words(0, 3, FIRST_WORDS_ROOM)
+        gather_bytes(0, 3, FIRST_BYTES_ROOM)
         permute(0, 1)
         permute_plane(0)
-        round_wb(0, on_scalar)
-        round_wb(1, on_scalar)
-        round_wb(2, on_scalar)
+        for e in range(3):
+            round_wb(e, on_scalar)
         first_product(0)
         round_wb(3, on_scalar)
-        gather_bytes(3, 6, 11)
+
+        gather_bytes(3, 6, RAW_PLANE_ROOM)
         permute(1, 3)
         first_product(1)
         first_product(2)
         round_wb(4, on_scalar)
         gather_words(3, 6, 1)
-        quantise(0, whole, ROOM * 1 + 0)
+        quantise(0, whole, ROOM * 1)
         permute(3, 4)
         first_product(3)
-        quantise(1, whole, ROOM * 10 + 512)
+        quantise(1, whole, own_place(1))
+
         permute_plane(1)
         permute(4, 7)
         first_product(4)
-        second_product(0, 0, C, on_scalar, 0 * C, 3 * C)
-        second_product(1, 0, C, on_scalar, 0 * C, 3 * C)
+        whole_y(0, on_scalar, 0, 2)
+        whole_y(1, on_scalar, 0, 2)
         gather_words(6, 8, 4)
-        quantise(2, whole, ROOM * 4 + 512)
+        quantise(2, whole, ROOM * 4 + PLANE)
         first_product(5)
-        second_product(2, 0, C, on_scalar, 0 * C, 3 * C)
+        whole_y(2, on_scalar, 2, 4)
         gather_bytes(6, 8, 4)
-        quantise(3, whole, ROOM * 4 + 3072)
-        second_product(3, 0, C, on_scalar, 3 * C, 5 * C)
+        quantise(3, whole, ROOM * 4 + BEHIND_WORDS)
+        whole_y(3, on_scalar, 2, 4)
         first_product(6)
-        quantise(4, whole, ROOM * 10 + 2048)
-        second_product(4, 0, C, on_scalar, 3 * C, 5 * C)
+        quantise(4, whole, own_place(4))
+        whole_y(4, on_scalar, 4, 5)
+
         round_wb(5, on_vector)
         round_wb(6, on_vector)
         permute(7, 8)
         first_product(7)
-        quantise(5, whole, ROOM * 10 + 2560)
-        second_product(5, 0, C, on_scalar, 5 * C, 6 * C)
-        quantise(6, whole, ROOM * 10 + 3072)
-        second_product(6, 0, C, on_scalar, 6 * C, 7 * C)
-        round_wb(7, on_vector)
-        quantise(7, [(C, C + N), (0, HALF), (HALF, C)], ROOM * 10 + 3584)
-        second_product(7, 0, HALF, on_scalar, 7 * C, 7 * C + HALF)
-        second_product(7, HALF, C, on_vector, 7 * C + HALF, 8 * C)
+        quantise(5, whole, own_place(5))
+        quantise(6, whole, own_place(6))
+        whole_y(5, on_vector, 5, 6)
+        whole_y(6, on_scalar, 6, 7)
+
+        last = E - 1
+        round_wb(last, on_vector)
+        quantise(last, [(C, C + N), (0, HALF), (HALF, C)], own_place(last))
+        for lo, copy in ((last * C, on_scalar), (last * C + HALF, on_vector)):
+            second_product(lo, lo + HALF, copy, lo, lo + HALF)

@@ -47,17 +47,14 @@ def tile_moe_elr_s_none_kernel(
         offsets = keep.tile([P, E * C // 16], U16, name="offsets")
         x_table = keep.tile([P, T], I32, name="x_table", align_bytes=ALIGN)
         x_plane = keep.tile([P, T], U8, name="x_plane", align_bytes=ALIGN)
-        wa_plane_raw = [
-            rooms.tile([P, H], U8, name="wa_plane_raw%d" % s, align_bytes=ALIGN, offset=ROOM * (RAW_PLANE_ROOM + s))
-            for s in sets
-        ]
+        wa_plane_raw = rooms.tile([P, H], U8, name="wa_plane_raw", align_bytes=ALIGN, offset=ROOM * RAW_PLANE_ROOM)
         wa_plane = [keep.tile([P, H], U8, name="wa_plane%d" % s, align_bytes=ALIGN) for s in sets]
         w_plane = keep.tile([P, E, N], U8, name="w_plane", align_bytes=ALIGN)
         w_codes = [keep.tile([P, SET, 2 * N], U8, name="w_codes%d" % s, align_bytes=ALIGN) for s in sets]
         rounded = [keep.tile([P, C + N, PACK], BF16, name="rounded%d" % e, align_bytes=ALIGN) for e in range(E)]
         wa_raw, wb_raw = {}, {}
 
-        for plane in (x_plane, wa_plane_raw[0], w_plane, wa_plane_raw[1]):
+        for plane in (x_plane, wa_plane[1], w_plane):
             nc.vector.memset(plane[:].bitcast(I32), 0)
 
         def load_x_plane():
@@ -66,11 +63,18 @@ def tile_moe_elr_s_none_kernel(
                     x_plane[r:P:QUADRANT, :].bitcast(I32), x_scales[0, r : ROWS * ROWS : ROWS, :].bitcast(I32)
                 )
 
-        def load_wa_plane(s):
+        def load_wa_plane():
             for q in range(ROWS):
                 nc.sync.dma_start(
-                    wa_plane_raw[s][QUADRANT * q : QUADRANT * q + SET * ROWS, :].bitcast(I32),
-                    wa_scales[SET * s : SET * (s + 1), 0, ROWS * q : ROWS * (q + 1), :].bitcast(I32),
+                    wa_plane_raw[QUADRANT * q : QUADRANT * (q + 1), :].bitcast(I32),
+                    wa_scales[:, 0, ROWS * q : ROWS * (q + 1), :].bitcast(I32),
+                )
+
+        def lower_wa_plane():
+            for q in range(ROWS):
+                nc.sync.dma_start(
+                    wa_plane[1][QUADRANT * q : QUADRANT * q + SET * ROWS, :].bitcast(I32),
+                    wa_plane[0][QUADRANT * q + SET * ROWS : QUADRANT * (q + 1), :].bitcast(I32),
                 )
 
         def load_w_plane():
@@ -105,19 +109,11 @@ def tile_moe_elr_s_none_kernel(
         for e in range(3):
             load_wb(e, e + 1)
         load_wa(0, 1)
-        load_wa_plane(0)
+        load_wa_plane()
         load_wb(3, 4)
         load_wa(1, 3)
         load_wb(4, 5)
         load_wa(3, 4)
-        load_wa_plane(1)
-        load_wa(4, 7)
-        load_w(0)
-        load_w_plane()
-        load_w(1)
-        load_wb(5, 7)
-        load_wa(7, 8)
-        load_wb(7, 8)
 
         out_view = out.rearrange("(b p) s -> p b s", p=P)
         slot_words, slot_plane, wa_codes, quantised, staged = {}, {}, {}, {}, {}
@@ -148,10 +144,10 @@ def tile_moe_elr_s_none_kernel(
             for e in range(first, end):
                 wa_codes[e] = codes[:, :, e - first, :]
 
-        def permute_plane(s):
+        def permute_plane():
             nc.vector.tensor_copy(
-                wa_plane[s][:].rearrange("p (t c i) -> p c t i", t=PACK, i=16),
-                wa_plane_raw[s][:].rearrange("p (c i t) -> p c t i", t=PACK, i=16),
+                wa_plane[0][:].rearrange("p (t c i) -> p c t i", t=PACK, i=16),
+                wa_plane_raw[:].rearrange("p (c i t) -> p c t i", t=PACK, i=16),
             )
 
         def round_wb(e, copy):
@@ -237,7 +233,16 @@ def tile_moe_elr_s_none_kernel(
         gather_words(0, 3, FIRST_WORDS_ROOM)
         gather_bytes(0, 3, FIRST_BYTES_ROOM)
         permute(0, 1)
-        permute_plane(0)
+        permute_plane()
+        lower_wa_plane()
+        load_wa(4, 7)
+        load_w(0)
+        load_w_plane()
+        load_w(1)
+        load_wb(5, 7)
+        load_wa(7, 8)
+        load_wb(7, 8)
+
         for e in range(3):
             round_wb(e, on_scalar)
         first_product(0)
@@ -254,7 +259,6 @@ def tile_moe_elr_s_none_kernel(
         first_product(3)
         quantise(1, whole, own_place(1))
 
-        permute_plane(1)
         permute(4, 7)
         first_product(4)
         whole_y(0, on_scalar, 0, 2)

@@ -104,10 +104,11 @@ def tile_moe_elr_s_none_kernel(
                 wb_raw[e] = rows[:, e - first, :]
 
         nc.sync.dma_start(offsets[:], offs)
-        nc.sync.dma_start(x_table[:], x_words[0].rearrange("p t d -> p (t d)").bitcast(I32))
+        load_wb(0, 1)
         load_x_plane()
-        for e in range(3):
-            load_wb(e, e + 1)
+        load_wb(1, 2)
+        nc.sync.dma_start(x_table[:], x_words[0].rearrange("p t d -> p (t d)").bitcast(I32))
+        load_wb(2, 3)
         load_wa(0, 1)
         load_wa_plane()
         load_wb(3, 4)
@@ -221,6 +222,36 @@ def tile_moe_elr_s_none_kernel(
             if end == store_end:
                 nc.sync.dma_start(out_view[:, :, store_first:store_end], y[:])
 
+        def last_product(e):
+            codes, plane = quantised[e]
+            groups = {}
+            for lo, b in [(lo, b) for lo in range(0, C, HALF) for b in range(N // P)]:
+                groups[lo, b] = psum.tile([P, HALF], F32, name="sums")
+                nc.tensor.matmul_mx(
+                    out=groups[lo, b][:],
+                    lhsT=w_codes[e // SET][:, e % SET, 2 * b * P : 2 * (b + 1) * P].bitcast(FP4X4),
+                    lhsT_scale=w_plane[:, e, b * P : (b + 1) * P],
+                    rhs=slot_words[e][:, lo : lo + HALF].bitcast(FP8X4),
+                    rhs_scale=slot_plane[e][:, lo : lo + HALF],
+                    start=True,
+                    stop=False,
+                )
+            for lo, copies in ((0, (on_scalar, on_scalar)), (HALF, (on_scalar, on_vector))):
+                y = keep.tile([P, N // P, HALF], F32, name="last_y%d" % lo)
+                for b, copy in enumerate(copies):
+                    wb_columns = slice(C + b * P, C + (b + 1) * P)
+                    nc.tensor.matmul_mx(
+                        out=groups[lo, b][:],
+                        lhsT=codes[:, wb_columns].bitcast(FP8X4),
+                        lhsT_scale=plane[:, wb_columns],
+                        rhs=codes[:, lo : lo + HALF].bitcast(FP8X4),
+                        rhs_scale=plane[:, lo : lo + HALF],
+                        start=False,
+                        stop=True,
+                    )
+                    copy(y[:, b, :], groups[lo, b][:])
+                nc.sync.dma_start(out_view[:, :, e * C + lo : e * C + lo + HALF], y[:])
+
         def whole_y(e, copy, store_first, store_end):
             second_product(e * C, (e + 1) * C, copy, store_first * C, store_end * C)
 
@@ -230,8 +261,9 @@ def tile_moe_elr_s_none_kernel(
         on_scalar, on_vector = nc.scalar.copy, nc.vector.tensor_copy
         whole = [(0, C + N)]
 
-        gather_words(0, 3, FIRST_WORDS_ROOM)
         gather_bytes(0, 3, FIRST_BYTES_ROOM)
+        gather_bytes(3, 4, 13)
+        gather_words(0, 3, FIRST_WORDS_ROOM)
         permute(0, 1)
         permute_plane()
         lower_wa_plane()
@@ -248,7 +280,7 @@ def tile_moe_elr_s_none_kernel(
         first_product(0)
         round_wb(3, on_scalar)
 
-        gather_bytes(3, 6, RAW_PLANE_ROOM)
+        gather_bytes(4, 6, RAW_PLANE_ROOM)
         permute(1, 3)
         first_product(1)
         first_product(2)
@@ -286,5 +318,4 @@ def tile_moe_elr_s_none_kernel(
         last = E - 1
         round_wb(last, on_vector)
         quantise(last, [(C, C + N), (0, HALF), (HALF, C)], own_place(last))
-        for lo, copy in ((last * C, on_scalar), (last * C + HALF, on_vector)):
-            second_product(lo, lo + HALF, copy, lo, lo + HALF)
+        last_product(last)

@@ -312,7 +312,7 @@ def tile_moe_elr_s_none_kernel(
         first_product(7)
         quantise(5, whole, own_place(5))
         quantise(6, whole, own_place(6))
-        whole_y(5, on_vector, 5, 6)
+        whole_y(5, on_scalar, 5, 6)
         whole_y(6, on_scalar, 6, 7)
 
         last = E - 1

@@ -22,16 +22,7 @@ HALF = 128
 SET = 4
 BANKS = 8
 ALIGN = 64
-
-ROOM = 4096
-FIRST_BYTES_ROOM, FIRST_WORDS_ROOM = 8, 9
-PLANES_ROOM = 10
-RAW_PLANE_ROOM = 11
-WB_ROOM = 20
-Y_ROOM = 28
-PLANE = C + N
-WORDS_AT = 1024
-BEHIND_WORDS = WORDS_AT + 2 * C * PACK
+ROOM = 8192
 
 
 def tile_moe_elr_s_none_kernel(
@@ -44,18 +35,31 @@ def tile_moe_elr_s_none_kernel(
         rooms = ctx.enter_context(tc.tile_pool(name="rooms", bufs=1))
         psum = ctx.enter_context(tc.psum_pool(name="psum", bufs=BANKS))
 
+        def sbuf(shape, dtype, name, place=None):
+            if place is None:
+                return keep.tile(shape, dtype, name=name, align_bytes=ALIGN)
+            return rooms.tile(shape, dtype, name=name, align_bytes=ALIGN, offset=ROOM * place[0] + place[1])
+
         offsets = keep.tile([P, E * C // 16], U16, name="offsets")
-        x_table = keep.tile([P, T], I32, name="x_table", align_bytes=ALIGN)
-        x_plane = keep.tile([P, T], U8, name="x_plane", align_bytes=ALIGN)
-        wa_plane_raw = rooms.tile([P, H], U8, name="wa_plane_raw", align_bytes=ALIGN, offset=ROOM * RAW_PLANE_ROOM)
-        wa_plane = [keep.tile([P, H], U8, name="wa_plane%d" % s, align_bytes=ALIGN) for s in sets]
-        w_plane = keep.tile([P, E, N], U8, name="w_plane", align_bytes=ALIGN)
-        w_codes = [keep.tile([P, SET, 2 * N], U8, name="w_codes%d" % s, align_bytes=ALIGN) for s in sets]
-        rounded = [keep.tile([P, C + N, PACK], BF16, name="rounded%d" % e, align_bytes=ALIGN) for e in range(E)]
-        wa_raw, wb_raw = {}, {}
+        x_table = sbuf([P, T], I32, "x_table")
+        x_plane = sbuf([P, T], U8, "x_plane")
+        wa_plane = [sbuf([P, H], U8, "wa_plane%d" % s) for s in sets]
+        w_plane = sbuf([P, E, N], U8, "w_plane")
+        w_codes = [sbuf([P, SET, 2 * N], U8, "w_codes%d" % s) for s in sets]
+        wa_raw, wb_raw, rounded = {}, {}, {}
+        slot_words, slot_plane, wa_codes, codes, planes, staged = {}, {}, {}, {}, {}, {}
+        raw_plane = {}
+        out_view = out.rearrange("(b p) s -> p b s", p=P)
+        on_scalar, on_vector = nc.scalar.copy, nc.vector.tensor_copy
 
         for plane in (x_plane, wa_plane[1], w_plane):
             nc.vector.memset(plane[:].bitcast(I32), 0)
+
+        def load_offsets():
+            nc.sync.dma_start(offsets[:], offs)
+
+        def load_x():
+            nc.sync.dma_start(x_table[:], x_words[0].rearrange("p t d -> p (t d)").bitcast(I32))
 
         def load_x_plane():
             for r in range(ROWS):
@@ -63,10 +67,11 @@ def tile_moe_elr_s_none_kernel(
                     x_plane[r:P:QUADRANT, :].bitcast(I32), x_scales[0, r : ROWS * ROWS : ROWS, :].bitcast(I32)
                 )
 
-        def load_wa_plane():
+        def load_wa_plane(place=None):
+            raw_plane[0] = sbuf([P, H], U8, "wa_plane_raw", place)
             for q in range(ROWS):
                 nc.sync.dma_start(
-                    wa_plane_raw[QUADRANT * q : QUADRANT * (q + 1), :].bitcast(I32),
+                    raw_plane[0][QUADRANT * q : QUADRANT * (q + 1), :].bitcast(I32),
                     wa_scales[:, 0, ROWS * q : ROWS * (q + 1), :].bitcast(I32),
                 )
 
@@ -90,232 +95,199 @@ def tile_moe_elr_s_none_kernel(
                 w_words[SET * s : SET * (s + 1), 0].rearrange("e p b -> p e b").bitcast(I32),
             )
 
-        def load_wa(first, end):
-            wa_raw[first] = rooms.tile(
-                [P, end - first, H], I32, name="wa_raw%d" % first, align_bytes=ALIGN, offset=ROOM * first
-            )
-            nc.sync.dma_start(wa_raw[first][:], wa_words[first:end, 0].rearrange("e p i d -> p e (i d)").bitcast(I32))
-
-        def load_wb(first, end):
-            place = ROOM * (WB_ROOM + first)
-            rows = rooms.tile([P, end - first, PACK * N], F32, name="wb_raw%d" % first, align_bytes=ALIGN, offset=place)
-            nc.sync.dma_start(rows[:], wb[first:end].rearrange("e (p j) n -> p e (j n)", j=PACK))
+        def load_wa(first, end, place=None):
+            raw = sbuf([P, end - first, H], I32, "wa_raw%d" % first, place)
+            nc.sync.dma_start(raw[:], wa_words[first:end, 0].rearrange("e p i d -> p e (i d)").bitcast(I32))
             for e in range(first, end):
-                wb_raw[e] = rows[:, e - first, :]
+                wa_raw[e] = raw[:, e - first, :]
 
-        nc.sync.dma_start(offsets[:], offs)
-        load_wb(0, 1)
-        load_x_plane()
-        load_wb(1, 2)
-        nc.sync.dma_start(x_table[:], x_words[0].rearrange("p t d -> p (t d)").bitcast(I32))
-        load_wb(2, 3)
-        load_wa(0, 1)
-        load_wa_plane()
-        load_wb(3, 4)
-        load_wa(1, 3)
-        load_wb(4, 5)
-        load_wa(3, 4)
+        def load_wb(first, end, place=None):
+            raw = sbuf([P, end - first, PACK * N], F32, "wb_raw%d" % first, place)
+            nc.sync.dma_start(raw[:], wb[first:end].rearrange("e (p j) n -> p e (j n)", j=PACK))
+            for e in range(first, end):
+                wb_raw[e] = raw[:, e - first, :]
 
-        out_view = out.rearrange("(b p) s -> p b s", p=P)
-        slot_words, slot_plane, wa_codes, quantised, staged = {}, {}, {}, {}, {}
-
-        def gather_words(first, end, room):
-            place = ROOM * room + WORDS_AT
-            words = rooms.tile([P, (end - first) * C], U32, name="slot_words%d" % first, align_bytes=ALIGN, offset=place)
-            entries = offsets[:, first * C // 16 : end * C // 16]
+        def gather_words(first, end, place=None):
+            words = sbuf([P, (end - first) * HALF], U32, "slot_words%d" % first, place)
+            entries = offsets[:, first * HALF // 16 : end * HALF // 16]
             nc.vector.tensor_copy(words[:], x_table[:].bitcast(U32).indirect(entries))
-            for e in range(first, end):
-                slot_words[e] = words[:, (e - first) * C : (e - first + 1) * C]
+            for u in range(first, end):
+                slot_words[u] = (words, (u - first) * HALF)
 
-        def gather_bytes(first, end, room):
-            scale_bytes = rooms.tile(
-                [P, (end - first) * C], U8, name="slot_plane%d" % first, align_bytes=ALIGN, offset=ROOM * room
-            )
-            entries = offsets[:, first * C // 16 : end * C // 16]
+        def gather_bytes(first, end, place=None):
+            scale_bytes = sbuf([P, (end - first) * HALF], U8, "slot_plane%d" % first, place)
+            entries = offsets[:, first * HALF // 16 : end * HALF // 16]
             nc.vector.tensor_copy(scale_bytes[:], x_plane[:].indirect(entries))
-            for e in range(first, end):
-                slot_plane[e] = scale_bytes[:, (e - first) * C : (e - first + 1) * C]
+            for u in range(first, end):
+                slot_plane[u] = (scale_bytes, (u - first) * HALF)
 
-        def permute(first, end):
-            codes = keep.tile([P, PACK, end - first, P], I32, name="wa_codes%d" % first, align_bytes=ALIGN)
+        def tokens(u, halves):
+            (words, at_w), (plane, at_p) = slot_words[u], slot_plane[u]
+            return words[:, at_w : at_w + halves * HALF].bitcast(FP8X4), plane[:, at_p : at_p + halves * HALF]
+
+        def permute(e, place=None):
+            wa_codes[e] = sbuf([P, PACK, P], I32, "wa_codes%d" % e, place)
             nc.vector.tensor_copy(
-                codes[:].rearrange("p (u v) e (c i) -> p (e c) u i v", v=2, i=4),
-                wa_raw[first][:].rearrange("p e (c i u v) -> p (e c) u i v", u=2, v=2, i=4),
+                wa_codes[e][:].rearrange("p (u v) (c i) -> p c u i v", v=2, i=4),
+                wa_raw[e].rearrange("p (c i u v) -> p c u i v", u=2, v=2, i=4),
             )
-            for e in range(first, end):
-                wa_codes[e] = codes[:, :, e - first, :]
 
         def permute_plane():
             nc.vector.tensor_copy(
                 wa_plane[0][:].rearrange("p (t c i) -> p c t i", t=PACK, i=16),
-                wa_plane_raw[:].rearrange("p (c i t) -> p c t i", t=PACK, i=16),
+                raw_plane[0][:].rearrange("p (c i t) -> p c t i", t=PACK, i=16),
             )
 
-        def round_wb(e, copy):
+        def input_of(e, place=None):
+            if e not in rounded:
+                rounded[e] = sbuf([P, C + N, PACK], BF16, "rounded%d" % e, place)
+            return rounded[e]
+
+        def round_wb(e, copy, lo=0, hi=N):
             copy(
-                rounded[e][:, C:, :].rearrange("p (c i) j -> p c j i", i=2),
-                wb_raw[e].rearrange("p (j c i) -> p c j i", j=PACK, i=2),
+                input_of(e)[:, C + lo : C + hi, :].rearrange("p (c i) j -> p c j i", i=2),
+                wb_raw[e].rearrange("p (j n) -> p j n", j=PACK)[:, :, lo:hi].rearrange("p j (c i) -> p c j i", i=2),
             )
 
-        def first_product(e):
+        def first_product(e, copy=on_scalar):
             first_row = ROWS * (e % SET)
-            for lo in range(0, C, HALF):
-                slots = slice(lo, lo + HALF)
+            for half in range(2):
+                words, plane = tokens(2 * e + half, 1)
                 h_sums = psum.tile([P, PACK, HALF], F32, name="sums")
                 for t in range(PACK):
                     nc.tensor.matmul_mx(
                         out=h_sums[:, t, :],
                         lhsT=wa_codes[e][:, t, :].bitcast(FP8X4),
                         lhsT_scale=wa_plane[e // SET][first_row:P, t * P : (t + 1) * P],
-                        rhs=slot_words[e][:, slots].bitcast(FP8X4),
-                        rhs_scale=slot_plane[e][:, slots],
+                        rhs=words,
+                        rhs_scale=plane,
                         start=True,
                         stop=True,
                     )
-                nc.scalar.copy(rounded[e][:, slots, :], h_sums[:].rearrange("p t s -> p s t"))
+                copy(input_of(e)[:, half * HALF : (half + 1) * HALF, :], h_sums[:].rearrange("p t s -> p s t"))
 
-        def quantise(e, pieces, place):
-            codes = keep.tile([P, C + N], U32, name="codes%d" % e, align_bytes=ALIGN)
-            plane = rooms.tile([P, PLANE], U8, name="plane%d" % e, align_bytes=ALIGN, offset=place)
-            for lo, hi in pieces:
-                nc.vector.quantize_mx(
-                    out=codes[:, lo:hi].bitcast(FP8X4),
-                    scales=plane[:, lo:hi],
-                    in_=rounded[e][:, lo:hi, :].rearrange("p c j -> p (c j)"),
-                )
-            quantised[e] = (codes, plane)
+        def quantise(e, lo=0, hi=C + N, place=None):
+            if e not in codes:
+                codes[e] = sbuf([P, C + N], U32, "codes%d" % e)
+                planes[e] = sbuf([P, C + N], U8, "plane%d" % e, place)
+            nc.vector.quantize_mx(
+                out=codes[e][:, lo:hi].bitcast(FP8X4),
+                scales=planes[e][:, lo:hi],
+                in_=rounded[e][:, lo:hi, :].rearrange("p c j -> p (c j)"),
+            )
 
-        def second_product(first, end, copy, store_first, store_end):
-            e = first // C
-            codes, plane = quantised[e]
-            y_sums = psum.tile([P, N // P, end - first], F32, name="sums")
+        def frozen_pass(e, b, group, first=0, halves=2):
+            words, plane = tokens(2 * e + first, halves)
+            nc.tensor.matmul_mx(
+                out=group,
+                lhsT=w_codes[e // SET][:, e % SET, 2 * b * P : 2 * (b + 1) * P].bitcast(FP4X4),
+                lhsT_scale=w_plane[:, e, b * P : (b + 1) * P],
+                rhs=words,
+                rhs_scale=plane,
+                start=True,
+                stop=False,
+            )
+
+        def adapter_pass(e, b, group, first=0, halves=2):
+            wb_columns = slice(C + b * P, C + (b + 1) * P)
+            slots = slice(first * HALF, (first + halves) * HALF)
+            nc.tensor.matmul_mx(
+                out=group,
+                lhsT=codes[e][:, wb_columns].bitcast(FP8X4),
+                lhsT_scale=planes[e][:, wb_columns],
+                rhs=codes[e][:, slots].bitcast(FP8X4),
+                rhs_scale=planes[e][:, slots],
+                start=False,
+                stop=True,
+            )
+
+        def second_product(e, copy, store_first, store_end, halves=2):
+            y_sums = psum.tile([P, N // P, C], F32, name="sums")
             for b in range(N // P):
-                wb_columns = slice(C + b * P, C + (b + 1) * P)
-                for lo in range(first, end, HALF):
-                    slots = slice(lo - e * C, lo - e * C + HALF)
-                    group = y_sums[:, b, lo - first : lo - first + HALF]
-                    nc.tensor.matmul_mx(
-                        out=group,
-                        lhsT=w_codes[e // SET][:, e % SET, 2 * b * P : 2 * (b + 1) * P].bitcast(FP4X4),
-                        lhsT_scale=w_plane[:, e, b * P : (b + 1) * P],
-                        rhs=slot_words[e][:, slots].bitcast(FP8X4),
-                        rhs_scale=slot_plane[e][:, slots],
-                        start=True,
-                        stop=False,
-                    )
-                    nc.tensor.matmul_mx(
-                        out=group,
-                        lhsT=codes[:, wb_columns].bitcast(FP8X4),
-                        lhsT_scale=plane[:, wb_columns],
-                        rhs=codes[:, slots].bitcast(FP8X4),
-                        rhs_scale=plane[:, slots],
-                        start=False,
-                        stop=True,
-                    )
-            if first == store_first:
-                place = ROOM * Y_ROOM + 4 * (N // P) * store_first
-                staged[store_first] = rooms.tile(
-                    [P, N // P, store_end - store_first], F32, name="y%d" % store_first, offset=place
-                )
+                for first in range(0, 2, halves):
+                    group = y_sums[:, b, first * HALF : (first + halves) * HALF]
+                    frozen_pass(e, b, group, first, halves)
+                    adapter_pass(e, b, group, first, halves)
+            if e == store_first:
+                staged[store_first] = sbuf([P, N // P, (store_end - store_first) * C], F32, "y%d" % e)
             y = staged[store_first]
-            copy(y[:, :, first - store_first : end - store_first], y_sums[:])
-            if end == store_end:
-                nc.sync.dma_start(out_view[:, :, store_first:store_end], y[:])
+            copy(y[:, :, (e - store_first) * C : (e + 1 - store_first) * C], y_sums[:])
+            if e + 1 == store_end:
+                nc.sync.dma_start(out_view[:, :, store_first * C : store_end * C], y[:])
 
-        def last_product(e):
-            codes, plane = quantised[e]
-            groups = {}
-            for lo, b in [(lo, b) for lo in range(0, C, HALF) for b in range(N // P)]:
-                groups[lo, b] = psum.tile([P, HALF], F32, name="sums")
-                nc.tensor.matmul_mx(
-                    out=groups[lo, b][:],
-                    lhsT=w_codes[e // SET][:, e % SET, 2 * b * P : 2 * (b + 1) * P].bitcast(FP4X4),
-                    lhsT_scale=w_plane[:, e, b * P : (b + 1) * P],
-                    rhs=slot_words[e][:, lo : lo + HALF].bitcast(FP8X4),
-                    rhs_scale=slot_plane[e][:, lo : lo + HALF],
-                    start=True,
-                    stop=False,
-                )
-            for lo, copies in ((0, (on_scalar, on_scalar)), (HALF, (on_scalar, on_vector))):
-                y = keep.tile([P, N // P, HALF], F32, name="last_y%d" % lo)
-                for b, copy in enumerate(copies):
-                    wb_columns = slice(C + b * P, C + (b + 1) * P)
-                    nc.tensor.matmul_mx(
-                        out=groups[lo, b][:],
-                        lhsT=codes[:, wb_columns].bitcast(FP8X4),
-                        lhsT_scale=plane[:, wb_columns],
-                        rhs=codes[:, lo : lo + HALF].bitcast(FP8X4),
-                        rhs_scale=plane[:, lo : lo + HALF],
-                        start=False,
-                        stop=True,
-                    )
-                    copy(y[:, b, :], groups[lo, b][:])
-                nc.sync.dma_start(out_view[:, :, e * C + lo : e * C + lo + HALF], y[:])
+        def last_product(e, copies):
+            groups = [psum.tile([P, C], F32, name="sums") for b in range(N // P)]
+            for b, group in enumerate(groups):
+                frozen_pass(e, b, group[:])
+            for b, group in enumerate(groups):
+                adapter_pass(e, b, group[:])
+                y = sbuf([P, C], F32, "last_y%d" % b)
+                copies[b](y[:], group[:])
+                nc.sync.dma_start(out_view[:, b, e * C : (e + 1) * C], y[:])
 
-        def whole_y(e, copy, store_first, store_end):
-            second_product(e * C, (e + 1) * C, copy, store_first * C, store_end * C)
+        load_offsets()
+        load_wa(0, 1)
+        load_x_plane()
+        load_wb(0, 1)
+        load_wb(1, 2)
+        load_wa_plane()
+        load_wb(2, 3)
+        load_x()
+        load_wb(3, 4)
+        load_wa(1, 3, (0, 0))
+        load_wa(3, 4)
 
-        def own_place(e):
-            return ROOM * PLANES_ROOM + PLANE * e
-
-        on_scalar, on_vector = nc.scalar.copy, nc.vector.tensor_copy
-        whole = [(0, C + N)]
-
-        gather_bytes(0, 3, FIRST_BYTES_ROOM)
-        gather_bytes(3, 4, 13)
-        gather_words(0, 3, FIRST_WORDS_ROOM)
-        permute(0, 1)
+        permute(0)
+        gather_bytes(0, 6)
+        gather_bytes(6, 12)
+        gather_bytes(12, 16)
         permute_plane()
         lower_wa_plane()
-        load_wa(4, 7)
+        load_wa(4, 6, (1, 0))
+        load_wa(6, 7)
         load_w(0)
-        load_w_plane()
         load_w(1)
-        load_wb(5, 7)
+        load_w_plane()
         load_wa(7, 8)
-        load_wb(7, 8)
+        load_wb(4, 6)
+        load_wb(6, 8)
 
         for e in range(3):
             round_wb(e, on_scalar)
+        gather_words(0, 1)
+        gather_words(1, 2)
+        gather_words(2, 8)
         first_product(0)
         round_wb(3, on_scalar)
-
-        gather_bytes(4, 6, RAW_PLANE_ROOM)
-        permute(1, 3)
-        first_product(1)
-        first_product(2)
-        round_wb(4, on_scalar)
-        gather_words(3, 6, 1)
-        quantise(0, whole, ROOM * 1)
-        permute(3, 4)
-        first_product(3)
-        quantise(1, whole, own_place(1))
-
-        permute(4, 7)
-        first_product(4)
-        whole_y(0, on_scalar, 0, 2)
-        whole_y(1, on_scalar, 0, 2)
-        gather_words(6, 8, 4)
-        quantise(2, whole, ROOM * 4 + PLANE)
-        first_product(5)
-        whole_y(2, on_scalar, 2, 4)
-        gather_bytes(6, 8, 4)
-        quantise(3, whole, ROOM * 4 + BEHIND_WORDS)
-        whole_y(3, on_scalar, 2, 4)
-        first_product(6)
-        quantise(4, whole, own_place(4))
-        whole_y(4, on_scalar, 4, 5)
-
-        round_wb(5, on_vector)
-        round_wb(6, on_vector)
-        permute(7, 8)
+        for e in range(1, 4):
+            permute(e)
+        gather_words(8, 12, (0, 1024))
+        for e in range(1, 4):
+            first_product(e)
+        quantise(0, place=(0, 0))
+        quantise(1, place=(0, 512))
+        for e in range(4, 7):
+            permute(e)
+        gather_words(12, 16, (1, 1024))
+        quantise(2, place=(1, 0))
+        quantise(3, place=(1, 512))
+        for e in range(4, 7):
+            first_product(e)
+        second_product(0, on_scalar, 0, 2, halves=1)
+        second_product(1, on_scalar, 0, 2)
+        second_product(2, on_scalar, 2, 4)
+        second_product(3, on_scalar, 2, 4)
+        permute(7)
         first_product(7)
-        quantise(5, whole, own_place(5))
-        quantise(6, whole, own_place(6))
-        whole_y(5, on_scalar, 5, 6)
-        whole_y(6, on_scalar, 6, 7)
-
-        last = E - 1
-        round_wb(last, on_vector)
-        quantise(last, [(C, C + N), (0, HALF), (HALF, C)], own_place(last))
-        last_product(last)
+        round_wb(4, on_vector)
+        round_wb(5, on_vector)
+        quantise(4)
+        quantise(5)
+        second_product(4, on_scalar, 4, 5)
+        second_product(5, on_scalar, 5, 6)
+        round_wb(6, on_vector)
+        round_wb(7, on_vector)
+        quantise(6)
+        quantise(7)
+        second_product(6, on_scalar, 6, 7)
+        last_product(7, (on_scalar, on_vector))

@@ -20,7 +20,7 @@ QUADRANT = 32
 ROWS = 4
 HALF = 128
 SET = 4
-BANKS = 8
+BANK = 2048
 ALIGN = 64
 ROOM = 8192
 
@@ -33,7 +33,7 @@ def tile_moe_elr_s_none_kernel(
     with ExitStack() as ctx:
         keep = ctx.enter_context(tc.tile_pool(name="keep", bufs=1))
         rooms = ctx.enter_context(tc.tile_pool(name="rooms", bufs=1))
-        psum = ctx.enter_context(tc.psum_pool(name="psum", bufs=BANKS))
+        psum = ctx.enter_context(tc.psum_pool(name="psum", bufs=1))
 
         def sbuf(shape, dtype, name, place=None):
             if place is None:
@@ -149,11 +149,11 @@ def tile_moe_elr_s_none_kernel(
                 wb_raw[e].rearrange("p (j n) -> p j n", j=PACK)[:, :, lo:hi].rearrange("p j (c i) -> p c j i", i=2),
             )
 
-        def first_product(e, copy=on_scalar):
+        def first_product(e, banks, copy=on_scalar):
             first_row = ROWS * (e % SET)
             for half in range(2):
                 words, plane = tokens(2 * e + half, 1)
-                h_sums = psum.tile([P, PACK, HALF], F32, name="sums")
+                h_sums = psum.tile([P, PACK, HALF], F32, name="h%d_%d" % (e, half), offset=BANK * banks[half])
                 for t in range(PACK):
                     nc.tensor.matmul_mx(
                         out=h_sums[:, t, :],
@@ -176,7 +176,7 @@ def tile_moe_elr_s_none_kernel(
                 in_=rounded[e][:, lo:hi, :].rearrange("p c j -> p (c j)"),
             )
 
-        def frozen_pass(e, b, group, first=0, halves=2):
+        def frozen_pass(e, b, group, first=0, halves=2, start=True):
             words, plane = tokens(2 * e + first, halves)
             nc.tensor.matmul_mx(
                 out=group,
@@ -184,11 +184,11 @@ def tile_moe_elr_s_none_kernel(
                 lhsT_scale=w_plane[:, e, b * P : (b + 1) * P],
                 rhs=words,
                 rhs_scale=plane,
-                start=True,
+                start=start,
                 stop=False,
             )
 
-        def adapter_pass(e, b, group, first=0, halves=2):
+        def adapter_pass(e, b, group, first=0, halves=2, stop=True):
             wb_columns = slice(C + b * P, C + (b + 1) * P)
             slots = slice(first * HALF, (first + halves) * HALF)
             nc.tensor.matmul_mx(
@@ -198,16 +198,17 @@ def tile_moe_elr_s_none_kernel(
                 rhs=codes[e][:, slots].bitcast(FP8X4),
                 rhs_scale=planes[e][:, slots],
                 start=False,
-                stop=True,
+                stop=stop,
             )
 
-        def second_product(e, copy, store_first, store_end, halves=2):
-            y_sums = psum.tile([P, N // P, C], F32, name="sums")
+        def second_product(e, bank, copy, store_first, store_end, halves=2):
+            y_sums = psum.tile([P, N // P, C], F32, name="y_sums%d" % e, offset=BANK * bank)
+            parts = [(b, first) for b in range(N // P) for first in range(0, 2, halves)]
+            for b, first in parts:
+                group = y_sums[:, b, first * HALF : (first + halves) * HALF]
+                frozen_pass(e, b, group, first, halves, (b, first) == parts[0])
             for b in range(N // P):
-                for first in range(0, 2, halves):
-                    group = y_sums[:, b, first * HALF : (first + halves) * HALF]
-                    frozen_pass(e, b, group, first, halves)
-                    adapter_pass(e, b, group, first, halves)
+                adapter_pass(e, b, y_sums[:, b, :], stop=b == N // P - 1)
             if e == store_first:
                 staged[store_first] = sbuf([P, N // P, (store_end - store_first) * C], F32, "y%d" % e)
             y = staged[store_first]
@@ -215,15 +216,20 @@ def tile_moe_elr_s_none_kernel(
             if e + 1 == store_end:
                 nc.sync.dma_start(out_view[:, :, store_first * C : store_end * C], y[:])
 
-        def last_product(e, copies):
-            groups = [psum.tile([P, C], F32, name="sums") for b in range(N // P)]
-            for b, group in enumerate(groups):
-                frozen_pass(e, b, group[:])
-            for b, group in enumerate(groups):
-                adapter_pass(e, b, group[:])
-                y = sbuf([P, C], F32, "last_y%d" % b)
-                copies[b](y[:], group[:])
-                nc.sync.dma_start(out_view[:, b, e * C : (e + 1) * C], y[:])
+        def last_product(e, banks):
+            groups = [(0, 0, 2, on_vector), (1, 0, 1, on_scalar), (1, 1, 1, on_vector)]
+            sums = []
+            for (b, first, halves, copy), bank in zip(groups, banks):
+                sums.append(psum.tile([P, halves * HALF], F32, name="last%d_%d" % (b, first), offset=BANK * bank))
+                frozen_pass(e, b, sums[-1][:], first, halves)
+            y = sbuf([P, N // P, C], F32, "y%d" % e)
+            for b in range(N // P):
+                quantise(e, C + b * P, C + (b + 1) * P)
+            for (b, first, halves, copy), group in zip(groups, sums):
+                adapter_pass(e, b, group[:], first, halves)
+                copy(y[:, b, first * HALF : (first + halves) * HALF], group[:])
+                if first + halves == 2:
+                    nc.sync.dma_start(out_view[:, b, e * C : (e + 1) * C], y[:, b, :])
 
         load_offsets()
         load_wa(0, 1)
@@ -250,44 +256,47 @@ def tile_moe_elr_s_none_kernel(
         load_w_plane()
         load_wa(7, 8)
         load_wb(4, 6)
-        load_wb(6, 8)
+        load_wb(6, 7)
+        load_wb(7, 8)
 
         for e in range(3):
             round_wb(e, on_scalar)
         gather_words(0, 1)
         gather_words(1, 2)
         gather_words(2, 8)
-        first_product(0)
+        first_product(0, (0, 1))
         round_wb(3, on_scalar)
         for e in range(1, 4):
             permute(e)
         gather_words(8, 12, (0, 1024))
         for e in range(1, 4):
-            first_product(e)
+            first_product(e, (2 * e, 2 * e + 1))
         quantise(0, place=(0, 0))
-        quantise(1, place=(0, 512))
         for e in range(4, 7):
             permute(e)
         gather_words(12, 16, (1, 1024))
+        quantise(1, place=(1, 3072))
         quantise(2, place=(1, 0))
         quantise(3, place=(1, 512))
-        for e in range(4, 7):
-            first_product(e)
-        second_product(0, on_scalar, 0, 2, halves=1)
-        second_product(1, on_scalar, 0, 2)
-        second_product(2, on_scalar, 2, 4)
-        second_product(3, on_scalar, 2, 4)
+        first_product(4, (0, 1))
+        first_product(5, (2, 3))
+        input_of(6, (2, 0))
+        first_product(6, (4, 5))
+        second_product(0, 6, on_scalar, 0, 2, halves=1)
+        second_product(1, 7, on_scalar, 0, 2)
+        second_product(2, 0, on_scalar, 2, 4)
+        second_product(3, 1, on_scalar, 2, 4)
         permute(7)
-        first_product(7)
+        first_product(7, (2, 3))
         round_wb(4, on_vector)
         round_wb(5, on_vector)
         quantise(4)
-        quantise(5)
-        second_product(4, on_scalar, 4, 5)
-        second_product(5, on_scalar, 5, 6)
         round_wb(6, on_vector)
-        round_wb(7, on_vector)
+        quantise(5)
         quantise(6)
-        quantise(7)
-        second_product(6, on_scalar, 6, 7)
-        last_product(7, (on_scalar, on_vector))
+        round_wb(7, on_vector)
+        quantise(7, 0, C, place=(2, 0))
+        second_product(4, 4, on_scalar, 4, 5)
+        second_product(5, 5, on_scalar, 5, 6)
+        second_product(6, 6, on_scalar, 6, 7)
+        last_product(7, (7, 0, 1))

@@ -105,7 +105,12 @@ def tile_moe_elr_s_none_kernel(
             raw = sbuf([P, end - first, PACK * N], F32, "wb_raw%d" % first, place)
             nc.sync.dma_start(raw[:], wb[first:end].rearrange("e (p j) n -> p e (j n)", j=PACK))
             for e in range(first, end):
-                wb_raw[e] = raw[:, e - first, :]
+                for lo in range(0, N, P):
+                    wb_raw[e, lo] = raw[:, e - first, :].rearrange("p (j n) -> p j n", j=PACK)[:, :, lo:]
+
+        def load_wb_columns(e, lo, hi, place=None):
+            wb_raw[e, lo] = sbuf([P, PACK, hi - lo], F32, "wb_raw%d_%d" % (e, lo), place)
+            nc.sync.dma_start(wb_raw[e, lo][:], wb[e].rearrange("(p j) n -> p j n", j=PACK)[:, :, lo:hi])
 
         def gather_words(first, end, place=None):
             words = sbuf([P, (end - first) * HALF], U32, "slot_words%d" % first, place)
@@ -138,15 +143,19 @@ def tile_moe_elr_s_none_kernel(
                 raw_plane[0][:].rearrange("p (c i t) -> p c t i", t=PACK, i=16),
             )
 
-        def input_of(e, place=None):
-            if e not in rounded:
-                rounded[e] = sbuf([P, C + N, PACK], BF16, "rounded%d" % e, place)
-            return rounded[e]
+        def input_of(e, lo, hi):
+            for first, tile in rounded[e]:
+                if first <= lo and hi <= first + tile.shape[1]:
+                    return tile[:, lo - first : hi - first, :]
+            raise ValueError("no tile holds these columns")
+
+        def make_input(e, lo=0, hi=C + N, place=None):
+            rounded.setdefault(e, []).append((lo, sbuf([P, hi - lo, PACK], BF16, "rounded%d_%d" % (e, lo), place)))
 
         def round_wb(e, copy, lo=0, hi=N):
             copy(
-                input_of(e)[:, C + lo : C + hi, :].rearrange("p (c i) j -> p c j i", i=2),
-                wb_raw[e].rearrange("p (j n) -> p j n", j=PACK)[:, :, lo:hi].rearrange("p j (c i) -> p c j i", i=2),
+                input_of(e, C + lo, C + hi).rearrange("p (c i) j -> p c j i", i=2),
+                wb_raw[e, lo][:, :, : hi - lo].rearrange("p j (c i) -> p c j i", i=2),
             )
 
         def first_product(e, banks, copy=on_scalar):
@@ -164,7 +173,7 @@ def tile_moe_elr_s_none_kernel(
                         start=True,
                         stop=True,
                     )
-                copy(input_of(e)[:, half * HALF : (half + 1) * HALF, :], h_sums[:].rearrange("p t s -> p s t"))
+                copy(input_of(e, half * HALF, (half + 1) * HALF), h_sums[:].rearrange("p t s -> p s t"))
 
         def quantise(e, lo=0, hi=C + N, place=None):
             if e not in codes:
@@ -173,7 +182,7 @@ def tile_moe_elr_s_none_kernel(
             nc.vector.quantize_mx(
                 out=codes[e][:, lo:hi].bitcast(FP8X4),
                 scales=planes[e][:, lo:hi],
-                in_=rounded[e][:, lo:hi, :].rearrange("p c j -> p (c j)"),
+                in_=input_of(e, lo, hi).rearrange("p c j -> p (c j)"),
             )
 
         def frozen_pass(e, b, group, first=0, halves=2, start=True):
@@ -237,35 +246,38 @@ def tile_moe_elr_s_none_kernel(
         load_wb(0, 1)
         load_wb(1, 2)
         load_wa_plane()
-        load_wb(2, 3)
         load_x()
-        load_wb(3, 4)
+        load_wb(2, 3)
         load_wa(1, 3, (0, 0))
         load_wa(3, 4)
 
         permute(0)
         gather_bytes(0, 6)
         gather_bytes(6, 12)
-        gather_bytes(12, 16)
         permute_plane()
         lower_wa_plane()
         load_wa(4, 6, (1, 0))
         load_wa(6, 7)
+        load_wb(3, 4)
         load_w(0)
-        load_w(1)
         load_w_plane()
         load_wa(7, 8)
         load_wb(4, 6)
+        load_w(1)
         load_wb(6, 7)
         load_wb(7, 8)
 
-        for e in range(3):
-            round_wb(e, on_scalar)
+        for e in (0, 1, 2, 3, 4, 7):
+            make_input(e)
+        make_input(5, place=(2, 0))
+        make_input(6, place=(3, 0))
+        round_wb(0, on_scalar)
+        round_wb(1, on_scalar)
         gather_words(0, 1)
         gather_words(1, 2)
         gather_words(2, 8)
         first_product(0, (0, 1))
-        round_wb(3, on_scalar)
+        round_wb(2, on_scalar)
         for e in range(1, 4):
             permute(e)
         gather_words(8, 12, (0, 1024))
@@ -274,29 +286,32 @@ def tile_moe_elr_s_none_kernel(
         quantise(0, place=(0, 0))
         for e in range(4, 7):
             permute(e)
+        gather_bytes(12, 16, (1, 3584))
         gather_words(12, 16, (1, 1024))
+        first_product(4, (0, 1))
+        round_wb(3, on_scalar, 0, P)
+        first_product(5, (2, 3))
         quantise(1, place=(1, 3072))
+        round_wb(3, on_vector, P, N)
         quantise(2, place=(1, 0))
         quantise(3, place=(1, 512))
-        first_product(4, (0, 1))
-        first_product(5, (2, 3))
-        input_of(6, (2, 0))
+        second_product(0, 4, on_scalar, 0, 2, halves=1)
+        second_product(1, 5, on_scalar, 0, 2)
+        second_product(2, 6, on_scalar, 2, 4)
+        second_product(3, 7, on_scalar, 2, 4)
         first_product(6, (4, 5))
-        second_product(0, 6, on_scalar, 0, 2, halves=1)
-        second_product(1, 7, on_scalar, 0, 2)
-        second_product(2, 0, on_scalar, 2, 4)
-        second_product(3, 1, on_scalar, 2, 4)
         permute(7)
-        first_product(7, (2, 3))
+        first_product(7, (6, 7))
         round_wb(4, on_vector)
         round_wb(5, on_vector)
         quantise(4)
-        round_wb(6, on_vector)
         quantise(5)
-        quantise(6)
+        round_wb(6, on_vector)
+        quantise(6, 0, C, place=(2, 0))
+        quantise(6, C, C + N)
         round_wb(7, on_vector)
-        quantise(7, 0, C, place=(2, 0))
-        second_product(4, 4, on_scalar, 4, 5)
-        second_product(5, 5, on_scalar, 5, 6)
-        second_product(6, 6, on_scalar, 6, 7)
-        last_product(7, (7, 0, 1))
+        quantise(7, 0, C, place=(3, 0))
+        second_product(4, 0, on_scalar, 4, 5)
+        second_product(5, 1, on_scalar, 5, 6)
+        second_product(6, 2, on_scalar, 6, 7)
+        last_product(7, (3, 4, 5))

@@ -175,6 +175,19 @@ def tile_moe_elr_s_none_kernel(
                     )
                 copy(input_of(e, half * HALF, (half + 1) * HALF), h_sums[:].rearrange("p t s -> p s t"))
 
+        def warm_up(bank):
+            unread = psum.tile([P, H], F32, name="warm_up", offset=BANK * bank)
+            for step in range(3):
+                nc.tensor.matmul_mx(
+                    out=unread[:],
+                    lhsT=wa_codes[0][:, 0, :].bitcast(FP8X4),
+                    lhsT_scale=raw_plane[0][:, :P],
+                    rhs=wa_raw[0].bitcast(FP8X4),
+                    rhs_scale=raw_plane[0][:],
+                    start=True,
+                    stop=True,
+                )
+
         def quantise(e, lo=0, hi=C + N, place=None):
             if e not in codes:
                 codes[e] = sbuf([P, C + N], U32, "codes%d" % e)
@@ -254,6 +267,7 @@ def tile_moe_elr_s_none_kernel(
         permute(0)
         gather_bytes(0, 6)
         gather_bytes(6, 12)
+        warm_up(7)
         permute_plane()
         lower_wa_plane()
         load_wa(4, 6, (1, 0))

@@ -275,10 +275,10 @@ def tile_moe_elr_s_none_kernel(
         load_wb(3, 4)
         load_w(0)
         load_w_plane()
-        load_wa(7, 8)
         load_wb(4, 6)
-        load_w(1)
+        load_wa(7, 8)
         load_wb(6, 7)
+        load_w(1)
         load_wb(7, 8)
 
         for e in (0, 1, 2, 3, 4, 7):
@@ -314,10 +314,10 @@ def tile_moe_elr_s_none_kernel(
         second_product(2, 6, on_scalar, 2, 4)
         second_product(3, 7, on_scalar, 2, 4)
         first_product(6, (4, 5))
-        permute(7)
-        first_product(7, (6, 7))
         round_wb(4, on_vector)
         round_wb(5, on_vector)
+        permute(7)
+        first_product(7, (6, 7))
         quantise(4)
         quantise(5)
         round_wb(6, on_vector)

@@ -154,8 +154,8 @@ def tile_moe_elr_s_none_kernel(
 
         def round_wb(e, copy, lo=0, hi=N):
             copy(
-                input_of(e, C + lo, C + hi).rearrange("p (c i) j -> p c j i", i=2),
-                wb_raw[e, lo][:, :, : hi - lo].rearrange("p j (c i) -> p c j i", i=2),
+                input_of(e, C + lo, C + hi).rearrange("p (c i) j -> p c j i", i=4),
+                wb_raw[e, lo][:, :, : hi - lo].rearrange("p j (c i) -> p c j i", i=4),
             )
 
         def first_product(e, banks, copy=on_scalar):

@@ -105,7 +105,7 @@ def tile_moe_elr_s_none_kernel(
             raw = sbuf([P, end - first, PACK * N], F32, "wb_raw%d" % first, place)
             nc.sync.dma_start(raw[:], wb[first:end].rearrange("e (p j) n -> p e (j n)", j=PACK))
             for e in range(first, end):
-                for lo in range(0, N, P):
+                for lo in range(0, N, P // 2):
                     wb_raw[e, lo] = raw[:, e - first, :].rearrange("p (j n) -> p j n", j=PACK)[:, :, lo:]
 
         def load_wb_columns(e, lo, hi, place=None):
@@ -303,10 +303,10 @@ def tile_moe_elr_s_none_kernel(
         gather_bytes(12, 16, (1, 3584))
         gather_words(12, 16, (1, 1024))
         first_product(4, (0, 1))
-        round_wb(3, on_scalar, 0, P)
+        round_wb(3, on_scalar, 0, 192)
         first_product(5, (2, 3))
         quantise(1, place=(1, 3072))
-        round_wb(3, on_vector, P, N)
+        round_wb(3, on_vector, 192, N)
         quantise(2, place=(1, 0))
         quantise(3, place=(1, 512))
         second_product(0, 4, on_scalar, 0, 2, halves=1)

@@ -130,11 +130,11 @@ def tile_moe_elr_s_none_kernel(
             (words, at_w), (plane, at_p) = slot_words[u], slot_plane[u]
             return words[:, at_w : at_w + halves * HALF].bitcast(FP8X4), plane[:, at_p : at_p + halves * HALF]
 
-        def permute(e, place=None):
-            wa_codes[e] = sbuf([P, PACK, P], I32, "wa_codes%d" % e, place)
+        def permute(e):
+            wa_codes[e] = sbuf([P, PACK, P], I32, "wa_codes%d" % e)
             nc.vector.tensor_copy(
-                wa_codes[e][:].rearrange("p (u v) (c i) -> p c u i v", v=2, i=4),
-                wa_raw[e].rearrange("p (c i u v) -> p c u i v", u=2, v=2, i=4),
+                wa_codes[e][:].rearrange("p t (c i) -> p c t i", i=2),
+                wa_raw[e].rearrange("p (c i t) -> p c t i", t=PACK, i=2),
             )
 
         def permute_plane():

from contextlib import ExitStack

import concourse.mybir as mybir

K, T, E, C, H, N = 512, 1024, 8, 256, 512, 256
FLOPS = 2 * E * C * (K * H + K * N + H * N)

F32 = mybir.dt.float32
BF16 = mybir.dt.bfloat16
I32 = mybir.dt.int32
U32 = mybir.dt.uint32
U16 = mybir.dt.uint16
U8 = mybir.dt.uint8
FP8X4 = mybir.dt.float8_e4m3fn_x4
FP4X4 = mybir.dt.float4_e2m1fn_x4

P = 128
PACK = 4
QUADRANT = 32
ROWS = 4
HALF = 128
SET = 4
BANK = 2048
ALIGN = 64
ROOM = 8192


def tile_moe_elr_s_none_kernel(
    tc, x_words, x_scales, w_words, w_scales, wa_words, wa_scales, wb, offs, out
):
    nc = tc.nc
    sets = range(E // SET)
    with ExitStack() as ctx:
        keep = ctx.enter_context(tc.tile_pool(name="keep", bufs=1))
        rooms = ctx.enter_context(tc.tile_pool(name="rooms", bufs=1))
        psum = ctx.enter_context(tc.psum_pool(name="psum", bufs=1))

        def sbuf(shape, dtype, name, place=None):
            if place is None:
                return keep.tile(shape, dtype, name=name, align_bytes=ALIGN)
            return rooms.tile(shape, dtype, name=name, align_bytes=ALIGN, offset=ROOM * place[0] + place[1])

        offsets = keep.tile([P, E * C // 16], U16, name="offsets")
        x_table = sbuf([P, T], I32, "x_table")
        x_plane = sbuf([P, T], U8, "x_plane")
        wa_plane = [sbuf([P, H], U8, "wa_plane%d" % s) for s in sets]
        w_plane = sbuf([P, E, N], U8, "w_plane")
        w_codes = [sbuf([P, SET, 2 * N], U8, "w_codes%d" % s) for s in sets]
        wa_raw, wb_raw, rounded = {}, {}, {}
        slot_words, slot_plane, wa_codes, codes, planes, staged = {}, {}, {}, {}, {}, {}
        raw_plane = {}
        out_view = out.rearrange("(b p) s -> p b s", p=P)
        on_scalar, on_vector = nc.scalar.copy, nc.vector.tensor_copy

        for plane in (x_plane, wa_plane[1], w_plane):
            nc.vector.memset(plane[:].bitcast(I32), 0)

        def load_offsets():
            nc.sync.dma_start(offsets[:], offs)

        def load_x():
            nc.sync.dma_start(x_table[:], x_words[0].rearrange("p t d -> p (t d)").bitcast(I32))

        def load_x_plane():
            for r in range(ROWS):
                nc.sync.dma_start(
                    x_plane[r:P:QUADRANT, :].bitcast(I32), x_scales[0, r : ROWS * ROWS : ROWS, :].bitcast(I32)
                )

        def load_wa_plane(place=None):
            raw_plane[0] = sbuf([P, H], U8, "wa_plane_raw", place)
            for q in range(ROWS):
                nc.sync.dma_start(
                    raw_plane[0][QUADRANT * q : QUADRANT * (q + 1), :].bitcast(I32),
                    wa_scales[:, 0, ROWS * q : ROWS * (q + 1), :].bitcast(I32),
                )

        def lower_wa_plane():
            for q in range(ROWS):
                nc.sync.dma_start(
                    wa_plane[1][QUADRANT * q : QUADRANT * q + SET * ROWS, :].bitcast(I32),
                    wa_plane[0][QUADRANT * q + SET * ROWS : QUADRANT * (q + 1), :].bitcast(I32),
                )

        def load_w_plane():
            for r in range(ROWS):
                nc.sync.dma_start(
                    w_plane[r:P:QUADRANT, :, :].bitcast(I32),
                    w_scales[:, 0, r : ROWS * ROWS : ROWS, :].rearrange("e q n -> q e n").bitcast(I32),
                )

        def load_w(s):
            nc.sync.dma_start(
                w_codes[s][:].bitcast(I32),
                w_words[SET * s : SET * (s + 1), 0].rearrange("e p b -> p e b").bitcast(I32),
            )

        def load_wa(first, end, place=None):
            raw = sbuf([P, end - first, H], I32, "wa_raw%d" % first, place)
            nc.sync.dma_start(raw[:], wa_words[first:end, 0].rearrange("e p i d -> p e (i d)").bitcast(I32))
            for e in range(first, end):
                wa_raw[e] = raw[:, e - first, :]

        def load_wb(first, end, place=None):
            raw = sbuf([P, end - first, PACK * N], F32, "wb_raw%d" % first, place)
            nc.sync.dma_start(raw[:], wb[first:end].rearrange("e (p j) n -> p e (j n)", j=PACK))
            for e in range(first, end):
                for lo in range(0, N, P // 2):
                    wb_raw[e, lo] = raw[:, e - first, :].rearrange("p (j n) -> p j n", j=PACK)[:, :, lo:]

        def load_wb_columns(e, lo, hi, place=None):
            wb_raw[e, lo] = sbuf([P, PACK, hi - lo], F32, "wb_raw%d_%d" % (e, lo), place)
            nc.sync.dma_start(wb_raw[e, lo][:], wb[e].rearrange("(p j) n -> p j n", j=PACK)[:, :, lo:hi])

        def gather_words(first, end, place=None):
            words = sbuf([P, (end - first) * HALF], U32, "slot_words%d" % first, place)
            entries = offsets[:, first * HALF // 16 : end * HALF // 16]
            nc.vector.tensor_copy(words[:], x_table[:].bitcast(U32).indirect(entries))
            for u in range(first, end):
                slot_words[u] = (words, (u - first) * HALF)

        def gather_bytes(first, end, place=None):
            scale_bytes = sbuf([P, (end - first) * HALF], U8, "slot_plane%d" % first, place)
            entries = offsets[:, first * HALF // 16 : end * HALF // 16]
            nc.vector.tensor_copy(scale_bytes[:], x_plane[:].indirect(entries))
            for u in range(first, end):
                slot_plane[u] = (scale_bytes, (u - first) * HALF)

        def tokens(u, halves):
            (words, at_w), (plane, at_p) = slot_words[u], slot_plane[u]
            return words[:, at_w : at_w + halves * HALF].bitcast(FP8X4), plane[:, at_p : at_p + halves * HALF]

        def permute(e):
            wa_codes[e] = sbuf([P, PACK, P], I32, "wa_codes%d" % e)
            nc.vector.tensor_copy(
                wa_codes[e][:].rearrange("p t (c i) -> p c t i", i=2),
                wa_raw[e].rearrange("p (c i t) -> p c t i", t=PACK, i=2),
            )

        def permute_plane():
            nc.vector.tensor_copy(
                wa_plane[0][:].rearrange("p (t c i) -> p c t i", t=PACK, i=16),
                raw_plane[0][:].rearrange("p (c i t) -> p c t i", t=PACK, i=16),
            )

        def input_of(e, lo, hi):
            for first, tile in rounded[e]:
                if first <= lo and hi <= first + tile.shape[1]:
                    return tile[:, lo - first : hi - first, :]
            raise ValueError("no tile holds these columns")

        def make_input(e, lo=0, hi=C + N, place=None):
            rounded.setdefault(e, []).append((lo, sbuf([P, hi - lo, PACK], BF16, "rounded%d_%d" % (e, lo), place)))

        def round_wb(e, copy, lo=0, hi=N):
            copy(
                input_of(e, C + lo, C + hi).rearrange("p (c i) j -> p c j i", i=4),
                wb_raw[e, lo][:, :, : hi - lo].rearrange("p j (c i) -> p c j i", i=4),
            )

        def first_product(e, banks, copy=on_scalar):
            first_row = ROWS * (e % SET)
            for half in range(2):
                words, plane = tokens(2 * e + half, 1)
                h_sums = psum.tile([P, PACK, HALF], F32, name="h%d_%d" % (e, half), offset=BANK * banks[half])
                for t in range(PACK):
                    nc.tensor.matmul_mx(
                        out=h_sums[:, t, :],
                        lhsT=wa_codes[e][:, t, :].bitcast(FP8X4),
                        lhsT_scale=wa_plane[e // SET][first_row:P, t * P : (t + 1) * P],
                        rhs=words,
                        rhs_scale=plane,
                        start=True,
                        stop=True,
                    )
                copy(input_of(e, half * HALF, (half + 1) * HALF), h_sums[:].rearrange("p t s -> p s t"))

        def warm_up(bank):
            unread = psum.tile([P, H], F32, name="warm_up", offset=BANK * bank)
            for step in range(3):
                nc.tensor.matmul_mx(
                    out=unread[:],
                    lhsT=wa_codes[0][:, 0, :].bitcast(FP8X4),
                    lhsT_scale=raw_plane[0][:, :P],
                    rhs=wa_raw[0].bitcast(FP8X4),
                    rhs_scale=raw_plane[0][:],
                    start=True,
                    stop=True,
                )

        def quantise(e, lo=0, hi=C + N, place=None):
            if e not in codes:
                codes[e] = sbuf([P, C + N], U32, "codes%d" % e)
                planes[e] = sbuf([P, C + N], U8, "plane%d" % e, place)
            nc.vector.quantize_mx(
                out=codes[e][:, lo:hi].bitcast(FP8X4),
                scales=planes[e][:, lo:hi],
                in_=input_of(e, lo, hi).rearrange("p c j -> p (c j)"),
            )

        def frozen_pass(e, b, group, first=0, halves=2, start=True):
            words, plane = tokens(2 * e + first, halves)
            nc.tensor.matmul_mx(
                out=group,
                lhsT=w_codes[e // SET][:, e % SET, 2 * b * P : 2 * (b + 1) * P].bitcast(FP4X4),
                lhsT_scale=w_plane[:, e, b * P : (b + 1) * P],
                rhs=words,
                rhs_scale=plane,
                start=start,
                stop=False,
            )

        def adapter_pass(e, b, group, first=0, halves=2, stop=True):
            wb_columns = slice(C + b * P, C + (b + 1) * P)
            slots = slice(first * HALF, (first + halves) * HALF)
            nc.tensor.matmul_mx(
                out=group,
                lhsT=codes[e][:, wb_columns].bitcast(FP8X4),
                lhsT_scale=planes[e][:, wb_columns],
                rhs=codes[e][:, slots].bitcast(FP8X4),
                rhs_scale=planes[e][:, slots],
                start=False,
                stop=stop,
            )

        def second_product(e, bank, copy, store_first, store_end, halves=2):
            y_sums = psum.tile([P, N // P, C], F32, name="y_sums%d" % e, offset=BANK * bank)
            parts = [(b, first) for b in range(N // P) for first in range(0, 2, halves)]
            for b, first in parts:
                group = y_sums[:, b, first * HALF : (first + halves) * HALF]
                frozen_pass(e, b, group, first, halves, (b, first) == parts[0])
            for b in range(N // P):
                adapter_pass(e, b, y_sums[:, b, :], stop=b == N // P - 1)
            if e == store_first:
                staged[store_first] = sbuf([P, N // P, (store_end - store_first) * C], F32, "y%d" % e)
            y = staged[store_first]
            copy(y[:, :, (e - store_first) * C : (e + 1 - store_first) * C], y_sums[:])
            if e + 1 == store_end:
                nc.sync.dma_start(out_view[:, :, store_first * C : store_end * C], y[:])

        def last_product(e, banks):
            groups = [(0, 0, 2, on_vector), (1, 0, 1, on_scalar), (1, 1, 1, on_vector)]
            sums = []
            for (b, first, halves, copy), bank in zip(groups, banks):
                sums.append(psum.tile([P, halves * HALF], F32, name="last%d_%d" % (b, first), offset=BANK * bank))
                frozen_pass(e, b, sums[-1][:], first, halves)
            y = sbuf([P, N // P, C], F32, "y%d" % e)
            for b in range(N // P):
                quantise(e, C + b * P, C + (b + 1) * P)
            for (b, first, halves, copy), group in zip(groups, sums):
                adapter_pass(e, b, group[:], first, halves)
                copy(y[:, b, first * HALF : (first + halves) * HALF], group[:])
                if first + halves == 2:
                    nc.sync.dma_start(out_view[:, b, e * C : (e + 1) * C], y[:, b, :])

        load_offsets()
        load_wa(0, 1)
        load_x_plane()
        load_wb(0, 1)
        load_wb(1, 2)
        load_wa_plane()
        load_x()
        load_wb(2, 3)
        load_wa(1, 3, (0, 0))
        load_wa(3, 4)

        permute(0)
        gather_bytes(0, 6)
        gather_bytes(6, 12)
        warm_up(7)
        permute_plane()
        lower_wa_plane()
        load_wa(4, 6, (1, 0))
        load_wa(6, 7)
        load_wb(3, 4)
        load_w(0)
        load_w_plane()
        load_wb(4, 6)
        load_wa(7, 8)
        load_wb(6, 7)
        load_w(1)
        load_wb(7, 8)

        for e in (0, 1, 2, 3, 4, 7):
            make_input(e)
        make_input(5, place=(2, 0))
        make_input(6, place=(3, 0))
        round_wb(0, on_scalar)
        round_wb(1, on_scalar)
        gather_words(0, 1)
        gather_words(1, 2)
        gather_words(2, 8)
        first_product(0, (0, 1))
        round_wb(2, on_scalar)
        for e in range(1, 4):
            permute(e)
        gather_words(8, 12, (0, 1024))
        for e in range(1, 4):
            first_product(e, (2 * e, 2 * e + 1))
        quantise(0, place=(0, 0))
        for e in range(4, 7):
            permute(e)
        gather_bytes(12, 16, (1, 3584))
        gather_words(12, 16, (1, 1024))
        first_product(4, (0, 1))
        round_wb(3, on_scalar, 0, 192)
        first_product(5, (2, 3))
        quantise(1, place=(1, 3072))
        round_wb(3, on_vector, 192, N)
        quantise(2, place=(1, 0))
        quantise(3, place=(1, 512))
        second_product(0, 4, on_scalar, 0, 2, halves=1)
        second_product(1, 5, on_scalar, 0, 2)
        second_product(2, 6, on_scalar, 2, 4)
        second_product(3, 7, on_scalar, 2, 4)
        first_product(6, (4, 5))
        round_wb(4, on_vector)
        round_wb(5, on_vector)
        permute(7)
        first_product(7, (6, 7))
        quantise(4)
        quantise(5)
        round_wb(6, on_vector)
        quantise(6, 0, C, place=(2, 0))
        quantise(6, C, C + N)
        round_wb(7, on_vector)
        quantise(7, 0, C, place=(3, 0))
        second_product(4, 0, on_scalar, 4, 5)
        second_product(5, 1, on_scalar, 5, 6)
        second_product(6, 2, on_scalar, 6, 7)
        last_product(7, (3, 4, 5))
